import numpy as np
import ml_dtypes


def mxq(x, axis, fmt="e4m3"):
    dtype, down = {"e4m3": (ml_dtypes.float8_e4m3fn, 7), "e5m2": (ml_dtypes.float8_e5m2, 14)}[fmt]
    v = np.moveaxis(np.asarray(x, np.float32).astype(ml_dtypes.bfloat16).astype(np.float64), axis, -1)
    blocks = v.reshape(v.shape[:-1] + (-1, 32))
    amax = np.abs(blocks).max(-1, keepdims=True)
    byte = np.maximum(np.where(amax > 0, np.frexp(amax)[1] - 1 + 127, 0) - down, 1)
    scale = np.exp2(byte - 127.0)
    codes = (blocks / scale).astype(np.float32).astype(dtype).astype(np.float64)
    return np.moveaxis((codes * scale).reshape(v.shape), -1, axis)


WIDE = False


def mx_kscale(k):
    if not WIDE:
        return np.ones(k)
    levels = np.array([10, -10, 5, -5, 0])
    if k % 512:
        return np.exp2(np.random.permutation(np.resize(levels, k // 32))).repeat(32)
    a = np.empty((k // 512, 16))
    for p in range(k // 512):
        a[p, :8] = np.random.permutation(np.resize(levels, 8))
        for g in range(8):
            far = levels[np.abs(levels - a[p, g]) >= 10]
            a[p, g + 8] = far[np.random.randint(len(far))]
    return np.exp2(a.ravel()).repeat(32)


def f64(x):
    return np.asarray(x).astype(np.float64)


def striped(idx):
    return np.tile(idx.reshape(-1, 16).T, (8, 1)).astype(np.uint16)


def unstriped(offs):
    return offs[:16].T.reshape(-1).astype(np.int64)


def pack_weight(w):
    k, n = w.shape
    w = f64(np.asarray(w, np.float32).astype(ml_dtypes.bfloat16)).reshape(k // 32, 32, n)
    amax = np.abs(w).max(1)
    byte = np.clip(np.where(amax > 0, np.frexp(amax)[1] - 1 + 127 - 7, 1), 1, 254)
    scaled = (w * np.exp2(127.0 - byte)[:, None, :]).reshape(k, n).astype(np.float32)
    words = np.ascontiguousarray(scaled.reshape(k // 512, 128, 4, n).transpose(0, 1, 3, 2)).astype(ml_dtypes.float8_e4m3fn).view(np.uint8)
    return words, np.ascontiguousarray(byte.astype(np.uint8).reshape(k // 512, 16, n))


def unpack_weight(words, scales):
    g, p, n, _ = words.shape
    vals = np.ascontiguousarray(words).view(ml_dtypes.float8_e4m3fn).astype(np.float64) * np.repeat(np.exp2(scales.astype(np.float64) - 127.0), 8, axis=1)[..., None]
    return vals.transpose(0, 1, 3, 2).reshape(g * 512, n)


K, T, S, V = 1024, 2048, 512, 512


def setup_inputs():
    n = np.random.standard_normal
    s = mx_kscale(K)[:, None]
    packed_xT = pack_weight(n((K, T)) * s)
    return {
        "x_words": packed_xT[0],
        "x_scales": packed_xT[1],
        "hT": (n((K, V)) / np.sqrt(K) / s).astype(np.float32),
        "gT": (n((K, V)) / np.sqrt(K) / s).astype(np.float32),
        "ka": (0.5 * n((V, 3)) + 0.3).astype(np.float32),
        "kb": (0.4 * n((V, 3))).astype(np.float32),
        "offs": striped(np.random.permutation(T)[:S]),
    }


def reference(x_words, x_scales, hT, gT, ka, kb, offs):
    hTq = mxq(f64(hT), 0, "e4m3")
    xq = unpack_weight(x_words, x_scales)[:, unstriped(offs)]
    y = hTq.T @ xq
    gTq = mxq(f64(gT), 0, "e4m3")
    z = gTq.T @ xq
    ww = f64(ka)[:, 0:1] * y + f64(ka)[:, 1:2] * (np.pad(y, ((0, 0), (1, 0)))[:, :S]) + f64(ka)[:, 2:3] * (np.pad(y, ((0, 0), (2, 0)))[:, :S]) + f64(kb)[:, 0:1] * z + f64(kb)[:, 1:2] * (np.pad(z, ((0, 0), (1, 0)))[:, :S]) + f64(kb)[:, 2:3] * (np.pad(z, ((0, 0), (2, 0)))[:, :S])
    ex = np.exp(ww - ww.max(axis=1, keepdims=True))
    return ex / ex.sum(axis=1, keepdims=True)

@@ -1,0 +1,170 @@
+from contextlib import ExitStack
+
+import concourse.mybir as mybir
+
+F32 = mybir.dt.float32
+BF16 = mybir.dt.bfloat16
+I32 = mybir.dt.int32
+U32 = mybir.dt.uint32
+U16 = mybir.dt.uint16
+U8 = mybir.dt.uint8
+FP8X4 = mybir.dt.float8_e4m3fn_x4
+ALU = mybir.AluOpType
+ACT = mybir.ActivationFunctionType
+AXIS = mybir.AxisListType
+
+K, T, S, V = 1024, 2048, 512, 512
+P = 128
+PACK = 4
+K_PASS = P * PACK
+PASSES = K // K_PASS
+TILES = V // P
+HALF = S // 2
+FLOPS = 2 * 2 * K * S * V
+
+
+def tile_picked_ymta_two_p_kernel(tc, x_words, x_scales, hT, gT, ka, kb, offs, out):
+    nc = tc.nc
+    with ExitStack() as ctx:
+        keep = ctx.enter_context(tc.tile_pool(name="keep", bufs=1))
+        psum = ctx.enter_context(tc.psum_pool(name="psum", bufs=1))
+
+        offsets = keep.tile([P, S // 16], U16, name="offsets")
+        word_table = [keep.tile([P, T], I32, name=f"word_table{o}", align_bytes=64) for o in range(PASSES)]
+        scale_table = keep.tile([P, T], U8, name="scale_table", align_bytes=64)
+        key_words = [keep.tile([P, S], U32, name=f"key_words{o}", align_bytes=64) for o in range(PASSES)]
+        key_scales = keep.tile([P, S], U8, name="key_scales", align_bytes=64)
+        taps_a = keep.tile([P, TILES, 8], F32, name="taps_a")
+        taps_b = keep.tile([P, TILES, 8], F32, name="taps_b")
+        warm = keep.tile([P, 8], F32, name="warm")
+        warm_out = keep.tile([P, 8], F32, name="warm_out")
+
+        raw = {}
+
+        def load_queries(name, src, i):
+            for o in range(PASSES):
+                tile = keep.tile([P, PACK, P], F32, name=f"raw_{name}{i}_{o}")
+                rows = src[o * K_PASS:(o + 1) * K_PASS, i * P:(i + 1) * P]
+                nc.sync.dma_start(out=tile[:], in_=rows.rearrange("(p j) w -> p j w", j=PACK))
+                raw[name, i, o] = tile
+
+        nc.vector.memset(scale_table[:].bitcast(I32), 0)
+        nc.vector.memset(warm[:], 0.0)
+        load_queries("h", hT, 0)
+        nc.sync.dma_start(offsets[:], offs)
+        for q in range(4):
+            nc.scalar.dma_start(
+                out=scale_table[32 * q:32 * q + 4 * PASSES, :].bitcast(I32),
+                in_=x_scales[:, 4 * q:4 * q + 4, :].bitcast(I32),
+            )
+        nc.scalar.activation(out=warm_out[:], in_=warm[:], func=ACT.Exp)
+        for o in range(PASSES):
+            nc.sync.dma_start(out=word_table[o][:], in_=x_words[o].rearrange("p n t -> p (n t)").bitcast(I32))
+        nc.sync.dma_start(out=taps_a[:, :, 0:3], in_=ka.rearrange("(i p) c -> p i c", p=P))
+        nc.sync.dma_start(out=taps_b[:, :, 0:3], in_=kb.rearrange("(i p) c -> p i c", p=P))
+        load_queries("g", gT, 0)
+        for i in range(1, TILES):
+            load_queries("h", hT, i)
+            load_queries("g", gT, i)
+
+        grouped, codes, scales, scores, acc, neg_max, expd, total, inv = {}, {}, {}, {}, {}, {}, {}, {}, {}
+
+        def cast(name, i, on_vector):
+            tile = keep.tile([P, PASSES, P, PACK], BF16, name=f"grouped_{name}{i}", align_bytes=64)
+            for o in range(PASSES):
+                dst = tile[:, o].rearrange("p (c i) t -> p c t i", i=4)
+                src = raw[name, i, o][:].rearrange("p t (c i) -> p c t i", i=4)
+                if on_vector:
+                    nc.vector.tensor_copy(out=dst, in_=src)
+                else:
+                    nc.scalar.copy(out=dst, in_=src)
+            grouped[name, i] = tile
+
+        def quantize(name, i):
+            codes[name, i] = keep.tile([P, PASSES * P], U32, name=f"codes_{name}{i}", align_bytes=64)
+            scales[name, i] = keep.tile([P, PASSES * P], U8, name=f"scales_{name}{i}", align_bytes=64)
+            nc.vector.quantize_mx(
+                out=codes[name, i][:].bitcast(FP8X4),
+                scales=scales[name, i][:],
+                in_=grouped[name, i][:].rearrange("p o w t -> p (o w t)"),
+            )
+
+        def product(name, i):
+            bank = psum.tile([P, S], F32, name=f"scores_{name}{i}")
+            for o in range(PASSES):
+                nc.tensor.matmul_mx(
+                    out=bank[:],
+                    lhsT=codes[name, i][:, o * P:(o + 1) * P].bitcast(FP8X4),
+                    lhsT_scale=scales[name, i][:, o * P:(o + 1) * P],
+                    rhs=key_words[o][:].bitcast(FP8X4),
+                    rhs_scale=key_scales[4 * o:P, :],
+                    start=(o == 0),
+                    stop=(o == PASSES - 1),
+                )
+            scores[name, i] = bank
+
+        def first_tap(i, on_vector):
+            acc[i] = keep.tile([P, S], F32, name=f"acc{i}")
+            if on_vector:
+                for lo in (0, HALF):
+                    nc.vector.tensor_scalar(acc[i][:, lo:lo + HALF], scores["h", i][:, lo:lo + HALF], taps_a[:, i, 0:1], None, ALU.mult)
+            else:
+                nc.scalar.activation(out=acc[i][:], in_=scores["h", i][:], func=ACT.Copy, scale=taps_a[:, i, 0:1])
+
+        def add_tap(name, taps, i, shift):
+            for lo in (0, HALF):
+                start = max(lo, shift)
+                cols = slice(start, lo + HALF)
+                nc.vector.scalar_tensor_tensor(
+                    out=acc[i][:, cols],
+                    in0=scores[name, i][:, start - shift:lo + HALF - shift],
+                    scalar=taps[:, i, shift:shift + 1],
+                    in1=acc[i][:, cols],
+                    op0=ALU.mult,
+                    op1=ALU.add,
+                )
+
+        def row_max(i):
+            neg_max[i] = keep.tile([P, 1], F32, name=f"neg_max{i}")
+            nc.vector.tensor_reduce(out=neg_max[i][:], in_=acc[i][:], axis=AXIS.X, op=ALU.max, negate=True)
+
+        def exponentiate(i):
+            expd[i] = keep.tile([P, S], F32, name=f"expd{i}")
+            total[i] = keep.tile([P, 1], F32, name=f"total{i}")
+            nc.scalar.activation(out=expd[i][:], in_=acc[i][:], func=ACT.Exp, bias=neg_max[i][:], accum_out=total[i][:])
+
+        def normalise(i, on_vector):
+            inv[i] = keep.tile([P, 1], F32, name=f"inv{i}")
+            nc.vector.reciprocal(out=inv[i][:], in_=total[i][:])
+            result = keep.tile([P, S], F32, name=f"result{i}")
+            if on_vector:
+                nc.vector.tensor_scalar(result[:], expd[i][:], inv[i][:], None, ALU.mult)
+            else:
+                nc.scalar.activation(out=result[:], in_=expd[i][:], func=ACT.Copy, scale=inv[i][:])
+            nc.sync.dma_start(out=out[i * P:(i + 1) * P, :], in_=result[:])
+
+        cast("h", 0, True)
+        quantize("h", 0)
+        nc.vector.tensor_copy(key_words[0][:], word_table[0][:].bitcast(U32).indirect(offsets[:]))
+        nc.vector.tensor_copy(key_scales[:], scale_table[:].indirect(offsets[:]))
+        nc.vector.tensor_copy(key_words[1][:], word_table[1][:].bitcast(U32).indirect(offsets[:]))
+
+        for i in range(TILES):
+            product("h", i)
+            cast("g", i, False)
+            quantize("g", i)
+            product("g", i)
+            first_tap(i, i == 0)
+            if i + 1 < TILES:
+                cast("h", i + 1, False)
+            add_tap("h", taps_a, i, 1)
+            add_tap("h", taps_a, i, 2)
+            if i > 0:
+                normalise(i - 1, False)
+            if i + 1 < TILES:
+                quantize("h", i + 1)
+            for shift in range(3):
+                add_tap("g", taps_b, i, shift)
+            row_max(i)
+            exponentiate(i)
+        normalise(TILES - 1, True)

@@ -1,6 +1,7 @@
 from contextlib import ExitStack
 
 import concourse.mybir as mybir
+from concourse.masks import make_identity
 
 F32 = mybir.dt.float32
 BF16 = mybir.dt.bfloat16
@@ -19,7 +20,8 @@ PACK = 4
 K_PASS = P * PACK
 PASSES = K // K_PASS
 TILES = V // P
-HALF = S // 2
+PAIR = 2
+TAPS = 3
 FLOPS = 2 * 2 * K * S * V
 
 
@@ -34,68 +36,80 @@ def tile_picked_ymta_two_p_kernel(tc, x_words, x_scales, hT, gT, ka, kb, offs, o
         scale_table = keep.tile([P, T], U8, name="scale_table", align_bytes=64)
         key_words = [keep.tile([P, S], U32, name=f"key_words{o}", align_bytes=64) for o in range(PASSES)]
         key_scales = keep.tile([P, S], U8, name="key_scales", align_bytes=64)
-        taps_a = keep.tile([P, TILES, 8], F32, name="taps_a")
-        taps_b = keep.tile([P, TILES, 8], F32, name="taps_b")
+        tap_rows = keep.tile([P, P * TAPS], F32, name="tap_rows")
+        taps = keep.tile([P, TAPS, 2 * TILES], F32, name="taps")
+        identity = keep.tile([P, P], F32, name="identity")
         warm = keep.tile([P, 8], F32, name="warm")
         warm_out = keep.tile([P, 8], F32, name="warm_out")
 
         raw = {}
 
-        def load_queries(name, src, i):
+        def load_queries(name, src, pair):
             for o in range(PASSES):
-                tile = keep.tile([P, PACK, P], F32, name=f"raw_{name}{i}_{o}")
-                rows = src[o * K_PASS:(o + 1) * K_PASS, i * P:(i + 1) * P]
+                tile = keep.tile([P, PACK, PAIR * P], F32, name=f"raw_{name}{pair}_{o}")
+                rows = src[o * K_PASS:(o + 1) * K_PASS, pair * PAIR * P:(pair + 1) * PAIR * P]
                 nc.sync.dma_start(out=tile[:], in_=rows.rearrange("(p j) w -> p j w", j=PACK))
-                raw[name, i, o] = tile
+                for m in range(PAIR):
+                    raw[name, pair * PAIR + m, o] = tile[:, :, m * P:(m + 1) * P]
 
-        nc.vector.memset(scale_table[:].bitcast(I32), 0)
+        nc.vector.memset(scale_table[:, 0:T // 2].bitcast(I32), 0)
+        nc.gpsimd.memset(scale_table[:, T // 2:T].bitcast(I32), 0)
         nc.vector.memset(warm[:], 0.0)
-        load_queries("h", hT, 0)
+        nc.vector.memset(tap_rows[:], 0.0)
+        make_identity(nc, identity[:])
+        nc.scalar.activation(out=warm_out[:], in_=warm[:], func=ACT.Exp)
+        nc.sync.dma_start(out=word_table[0][:], in_=x_words[0].rearrange("p n t -> p (n t)").bitcast(I32))
         nc.sync.dma_start(offsets[:], offs)
+        nc.sync.dma_start(out=word_table[1][:], in_=x_words[1].rearrange("p n t -> p (n t)").bitcast(I32))
         for q in range(4):
-            nc.scalar.dma_start(
+            nc.sync.dma_start(
                 out=scale_table[32 * q:32 * q + 4 * PASSES, :].bitcast(I32),
                 in_=x_scales[:, 4 * q:4 * q + 4, :].bitcast(I32),
             )
-        nc.scalar.activation(out=warm_out[:], in_=warm[:], func=ACT.Exp)
-        for o in range(PASSES):
-            nc.sync.dma_start(out=word_table[o][:], in_=x_words[o].rearrange("p n t -> p (n t)").bitcast(I32))
-        nc.sync.dma_start(out=taps_a[:, :, 0:3], in_=ka.rearrange("(i p) c -> p i c", p=P))
-        nc.sync.dma_start(out=taps_b[:, :, 0:3], in_=kb.rearrange("(i p) c -> p i c", p=P))
-        load_queries("g", gT, 0)
-        for i in range(1, TILES):
-            load_queries("h", hT, i)
-            load_queries("g", gT, i)
+        nc.sync.dma_start(out=tap_rows[0:TILES, :], in_=ka.rearrange("(i p) c -> i (p c)", p=P))
+        nc.sync.dma_start(out=tap_rows[TILES:2 * TILES, :], in_=kb.rearrange("(i p) c -> i (p c)", p=P))
+
+        turned = psum.tile([P, TAPS, P], F32, name="turned", tag=f"scores_g{TILES - 1}")
+        for c in range(TAPS):
+            nc.tensor.transpose(turned[:, c, :], tap_rows[:, c::TAPS], identity[:])
+        nc.scalar.copy(out=taps[:], in_=turned[:, :, 0:2 * TILES])
+
+        for pair in range(TILES // PAIR):
+            load_queries("h", hT, pair)
+            load_queries("g", gT, pair)
+
+        def tap(name, i, shift):
+            col = i if name == "h" else TILES + i
+            return taps[:, shift, col:col + 1]
 
         grouped, codes, scales, scores, acc, neg_max, expd, total, inv = {}, {}, {}, {}, {}, {}, {}, {}, {}
 
-        def cast(name, i, on_vector):
-            tile = keep.tile([P, PASSES, P, PACK], BF16, name=f"grouped_{name}{i}", align_bytes=64)
-            for o in range(PASSES):
-                dst = tile[:, o].rearrange("p (c i) t -> p c t i", i=4)
-                src = raw[name, i, o][:].rearrange("p t (c i) -> p c t i", i=4)
-                if on_vector:
-                    nc.vector.tensor_copy(out=dst, in_=src)
-                else:
-                    nc.scalar.copy(out=dst, in_=src)
-            grouped[name, i] = tile
+        def cast(name, i, o, on_vector):
+            tile = keep.tile([P, P, PACK], BF16, name=f"grouped_{name}{i}_{o}", align_bytes=64)
+            dst = tile[:].rearrange("p (c i) t -> p c t i", i=4)
+            src = raw[name, i, o].rearrange("p t (c i) -> p c t i", i=4)
+            if on_vector:
+                nc.vector.tensor_copy(out=dst, in_=src)
+            else:
+                nc.scalar.copy(out=dst, in_=src)
+            grouped[name, i, o] = tile
 
-        def quantize(name, i):
-            codes[name, i] = keep.tile([P, PASSES * P], U32, name=f"codes_{name}{i}", align_bytes=64)
-            scales[name, i] = keep.tile([P, PASSES * P], U8, name=f"scales_{name}{i}", align_bytes=64)
+        def quantize(name, i, o):
+            codes[name, i, o] = keep.tile([P, P], U32, name=f"codes_{name}{i}_{o}", align_bytes=64)
+            scales[name, i, o] = keep.tile([P, P], U8, name=f"scales_{name}{i}_{o}", align_bytes=64)
             nc.vector.quantize_mx(
-                out=codes[name, i][:].bitcast(FP8X4),
-                scales=scales[name, i][:],
-                in_=grouped[name, i][:].rearrange("p o w t -> p (o w t)"),
+                out=codes[name, i, o][:].bitcast(FP8X4),
+                scales=scales[name, i, o][:],
+                in_=grouped[name, i, o][:].rearrange("p w t -> p (w t)"),
             )
 
         def product(name, i):
-            bank = psum.tile([P, S], F32, name=f"scores_{name}{i}")
+            bank = psum.tile([P, S], F32, name=f"scores_{name}{i}", tag=f"scores_{name}{i}")
             for o in range(PASSES):
                 nc.tensor.matmul_mx(
                     out=bank[:],
-                    lhsT=codes[name, i][:, o * P:(o + 1) * P].bitcast(FP8X4),
-                    lhsT_scale=scales[name, i][:, o * P:(o + 1) * P],
+                    lhsT=codes[name, i, o][:].bitcast(FP8X4),
+                    lhsT_scale=scales[name, i, o][:],
                     rhs=key_words[o][:].bitcast(FP8X4),
                     rhs_scale=key_scales[4 * o:P, :],
                     start=(o == 0),
@@ -106,23 +120,19 @@ def tile_picked_ymta_two_p_kernel(tc, x_words, x_scales, hT, gT, ka, kb, offs, o
         def first_tap(i, on_vector):
             acc[i] = keep.tile([P, S], F32, name=f"acc{i}")
             if on_vector:
-                for lo in (0, HALF):
-                    nc.vector.tensor_scalar(acc[i][:, lo:lo + HALF], scores["h", i][:, lo:lo + HALF], taps_a[:, i, 0:1], None, ALU.mult)
+                nc.vector.tensor_scalar(acc[i][:], scores["h", i][:], tap("h", i, 0), None, ALU.mult)
             else:
-                nc.scalar.activation(out=acc[i][:], in_=scores["h", i][:], func=ACT.Copy, scale=taps_a[:, i, 0:1])
+                nc.scalar.activation(out=acc[i][:], in_=scores["h", i][:], func=ACT.Copy, scale=tap("h", i, 0))
 
-        def add_tap(name, taps, i, shift):
-            for lo in (0, HALF):
-                start = max(lo, shift)
-                cols = slice(start, lo + HALF)
-                nc.vector.scalar_tensor_tensor(
-                    out=acc[i][:, cols],
-                    in0=scores[name, i][:, start - shift:lo + HALF - shift],
-                    scalar=taps[:, i, shift:shift + 1],
-                    in1=acc[i][:, cols],
-                    op0=ALU.mult,
-                    op1=ALU.add,
-                )
+        def add_tap(name, i, shift):
+            nc.vector.scalar_tensor_tensor(
+                out=acc[i][:, shift:S],
+                in0=scores[name, i][:, 0:S - shift],
+                scalar=tap(name, i, shift),
+                in1=acc[i][:, shift:S],
+                op0=ALU.mult,
+                op1=ALU.add,
+            )
 
         def row_max(i):
             neg_max[i] = keep.tile([P, 1], F32, name=f"neg_max{i}")
@@ -143,28 +153,40 @@ def tile_picked_ymta_two_p_kernel(tc, x_words, x_scales, hT, gT, ka, kb, offs, o
                 nc.scalar.activation(out=result[:], in_=expd[i][:], func=ACT.Copy, scale=inv[i][:])
             nc.sync.dma_start(out=out[i * P:(i + 1) * P, :], in_=result[:])
 
-        cast("h", 0, True)
-        quantize("h", 0)
         nc.vector.tensor_copy(key_words[0][:], word_table[0][:].bitcast(U32).indirect(offsets[:]))
-        nc.vector.tensor_copy(key_scales[:], scale_table[:].indirect(offsets[:]))
         nc.vector.tensor_copy(key_words[1][:], word_table[1][:].bitcast(U32).indirect(offsets[:]))
+        nc.vector.tensor_copy(key_scales[:], scale_table[:].indirect(offsets[:]))
 
-        for i in range(TILES):
-            product("h", i)
-            cast("g", i, False)
-            quantize("g", i)
-            product("g", i)
-            first_tap(i, i == 0)
-            if i + 1 < TILES:
-                cast("h", i + 1, False)
-            add_tap("h", taps_a, i, 1)
-            add_tap("h", taps_a, i, 2)
-            if i > 0:
-                normalise(i - 1, False)
-            if i + 1 < TILES:
-                quantize("h", i + 1)
-            for shift in range(3):
-                add_tap("g", taps_b, i, shift)
-            row_max(i)
-            exponentiate(i)
-        normalise(TILES - 1, True)
+        on_vector = {("h", 0, 0), ("h", 0, 1)}
+
+        def operands(name, pair):
+            tiles = range(pair * PAIR, (pair + 1) * PAIR)
+            for o in range(PASSES):
+                for i in tiles:
+                    cast(name, i, o, (name, i, o) in on_vector)
+                    quantize(name, i, o)
+            for i in tiles:
+                product(name, i)
+
+        operands("h", 0)
+        for pair in range(TILES // PAIR):
+            tiles = range(pair * PAIR, (pair + 1) * PAIR)
+            for i in tiles:
+                first_tap(i, i == 0)
+            operands("g", pair)
+            for shift in (1, 2):
+                for i in tiles:
+                    add_tap("h", i, shift)
+            if pair > 0:
+                for i in tiles:
+                    normalise(i - PAIR, False)
+            if pair + 1 < TILES // PAIR:
+                operands("h", pair + 1)
+            for shift in range(TAPS):
+                for i in tiles:
+                    add_tap("g", i, shift)
+            for i in tiles:
+                row_max(i)
+                exponentiate(i)
+        for i in range(TILES - PAIR, TILES):
+            normalise(i, True)

@@ -44,39 +44,54 @@ def tile_picked_ymta_two_p_kernel(tc, x_words, x_scales, hT, gT, ka, kb, offs, o
 
         raw = {}
 
-        def load_queries(name, src, pair):
-            for o in range(PASSES):
-                tile = keep.tile([P, PACK, PAIR * P], F32, name=f"raw_{name}{pair}_{o}")
-                rows = src[o * K_PASS:(o + 1) * K_PASS, pair * PAIR * P:(pair + 1) * PAIR * P]
-                nc.sync.dma_start(out=tile[:], in_=rows.rearrange("(p j) w -> p j w", j=PACK))
-                for m in range(PAIR):
-                    raw[name, pair * PAIR + m, o] = tile[:, :, m * P:(m + 1) * P]
+        def load_queries(name, first, count, o):
+            src = hT if name == "h" else gT
+            tile = keep.tile([P, PACK, count * P], F32, name=f"raw_{name}{first}_{o}")
+            rows = src[o * K_PASS:(o + 1) * K_PASS, first * P:(first + count) * P]
+            nc.sync.dma_start(out=tile[:], in_=rows.rearrange("(p j) w -> p j w", j=PACK))
+            for m in range(count):
+                raw[name, first + m, o] = (tile, m * P)
 
-        nc.vector.memset(scale_table[:, 0:T // 2].bitcast(I32), 0)
-        nc.gpsimd.memset(scale_table[:, T // 2:T].bitcast(I32), 0)
+        def load_words(o):
+            nc.sync.dma_start(out=word_table[o][:], in_=x_words[o].rearrange("p n t -> p (n t)").bitcast(I32))
+
+        def load_scales(o):
+            for q in range(4):
+                nc.sync.dma_start(
+                    out=scale_table[32 * q + 4 * o:32 * q + 4 * o + 4, :].bitcast(I32),
+                    in_=x_scales[o, 4 * q:4 * q + 4, :].bitcast(I32),
+                )
+
+        def load_taps():
+            nc.sync.dma_start(out=tap_rows[0:TILES, :], in_=ka.rearrange("(i p) c -> i (p c)", p=P))
+            nc.sync.dma_start(out=tap_rows[TILES:2 * TILES, :], in_=kb.rearrange("(i p) c -> i (p c)", p=P))
+
+        nc.gpsimd.memset(scale_table[:].bitcast(I32), 0)
+        nc.gpsimd.memset(tap_rows[:], 0.0)
         nc.vector.memset(warm[:], 0.0)
-        nc.vector.memset(tap_rows[:], 0.0)
+        minus_one = keep.tile([P, 1], F32, name="minus_one")
+        nc.gpsimd.memset(minus_one[:], -1.0)
         make_identity(nc, identity[:])
         nc.scalar.activation(out=warm_out[:], in_=warm[:], func=ACT.Exp)
-        nc.sync.dma_start(out=word_table[0][:], in_=x_words[0].rearrange("p n t -> p (n t)").bitcast(I32))
+        load_queries("h", 0, 2, 0)
         nc.sync.dma_start(offsets[:], offs)
-        nc.sync.dma_start(out=word_table[1][:], in_=x_words[1].rearrange("p n t -> p (n t)").bitcast(I32))
-        for q in range(4):
-            nc.sync.dma_start(
-                out=scale_table[32 * q:32 * q + 4 * PASSES, :].bitcast(I32),
-                in_=x_scales[:, 4 * q:4 * q + 4, :].bitcast(I32),
-            )
-        nc.sync.dma_start(out=tap_rows[0:TILES, :], in_=ka.rearrange("(i p) c -> i (p c)", p=P))
-        nc.sync.dma_start(out=tap_rows[TILES:2 * TILES, :], in_=kb.rearrange("(i p) c -> i (p c)", p=P))
+        load_scales(0)
+        load_words(0)
+        load_scales(1)
+        load_taps()
+        load_words(1)
+        load_queries("h", 0, 2, 1)
+        load_queries("g", 0, 2, 0)
+        load_queries("g", 0, 2, 1)
+        load_queries("h", 2, 2, 0)
+        load_queries("h", 2, 2, 1)
+        load_queries("g", 2, 2, 0)
+        load_queries("g", 2, 2, 1)
 
         turned = psum.tile([P, TAPS, P], F32, name="turned", tag=f"scores_g{TILES - 1}")
         for c in range(TAPS):
             nc.tensor.transpose(turned[:, c, :], tap_rows[:, c::TAPS], identity[:])
         nc.scalar.copy(out=taps[:], in_=turned[:, :, 0:2 * TILES])
-
-        for pair in range(TILES // PAIR):
-            load_queries("h", hT, pair)
-            load_queries("g", gT, pair)
 
         def tap(name, i, shift):
             col = i if name == "h" else TILES + i
@@ -84,38 +99,45 @@ def tile_picked_ymta_two_p_kernel(tc, x_words, x_scales, hT, gT, ka, kb, offs, o
 
         grouped, codes, scales, scores, acc, neg_max, expd, total, inv = {}, {}, {}, {}, {}, {}, {}, {}, {}
 
-        def cast(name, i, o, on_vector):
-            tile = keep.tile([P, P, PACK], BF16, name=f"grouped_{name}{i}_{o}", align_bytes=64)
-            dst = tile[:].rearrange("p (c i) t -> p c t i", i=4)
-            src = raw[name, i, o].rearrange("p t (c i) -> p c t i", i=4)
-            if on_vector:
-                nc.vector.tensor_copy(out=dst, in_=src)
+        def cast(name, first, count, o, engine):
+            tile = keep.tile([P, count * P, PACK], BF16, name=f"grouped_{name}{first}_{o}", align_bytes=64)
+            loaded, at = raw[name, first, o]
+            rows = loaded[:, :, at:at + count * P]
+            if engine == "gpsimd":
+                nc.gpsimd.tensor_scalar(tile[:], rows.rearrange("p t w -> p w t"), 1.0, 0.0, ALU.mult, ALU.add)
             else:
-                nc.scalar.copy(out=dst, in_=src)
-            grouped[name, i, o] = tile
+                dst = tile[:].rearrange("p (c i) t -> p c t i", i=4)
+                src = rows.rearrange("p t (c i) -> p c t i", i=4)
+                if engine == "vector":
+                    nc.vector.tensor_copy(out=dst, in_=src)
+                else:
+                    nc.scalar.copy(out=dst, in_=src)
+            grouped[name, first, o] = tile
 
-        def quantize(name, i, o):
-            codes[name, i, o] = keep.tile([P, P], U32, name=f"codes_{name}{i}_{o}", align_bytes=64)
-            scales[name, i, o] = keep.tile([P, P], U8, name=f"scales_{name}{i}_{o}", align_bytes=64)
+        def quantize(name, first, count, o):
+            words = keep.tile([P, count * P], U32, name=f"codes_{name}{first}_{o}", align_bytes=64)
+            plane = keep.tile([P, count * P], U8, name=f"scales_{name}{first}_{o}", align_bytes=64)
             nc.vector.quantize_mx(
-                out=codes[name, i, o][:].bitcast(FP8X4),
-                scales=scales[name, i, o][:],
-                in_=grouped[name, i, o][:].rearrange("p w t -> p (w t)"),
+                out=words[:].bitcast(FP8X4),
+                scales=plane[:],
+                in_=grouped[name, first, o][:].rearrange("p w t -> p (w t)"),
             )
+            for m in range(count):
+                codes[name, first + m, o] = words[:, m * P:(m + 1) * P]
+                scales[name, first + m, o] = plane[:, m * P:(m + 1) * P]
 
-        def product(name, i):
-            bank = psum.tile([P, S], F32, name=f"scores_{name}{i}", tag=f"scores_{name}{i}")
-            for o in range(PASSES):
-                nc.tensor.matmul_mx(
-                    out=bank[:],
-                    lhsT=codes[name, i, o][:].bitcast(FP8X4),
-                    lhsT_scale=scales[name, i, o][:],
-                    rhs=key_words[o][:].bitcast(FP8X4),
-                    rhs_scale=key_scales[4 * o:P, :],
-                    start=(o == 0),
-                    stop=(o == PASSES - 1),
-                )
-            scores[name, i] = bank
+        def product(name, i, o):
+            if o == 0:
+                scores[name, i] = psum.tile([P, S], F32, name=f"scores_{name}{i}", tag=f"scores_{name}{i}")
+            nc.tensor.matmul_mx(
+                out=scores[name, i][:],
+                lhsT=codes[name, i, o].bitcast(FP8X4),
+                lhsT_scale=scales[name, i, o],
+                rhs=key_words[o][:].bitcast(FP8X4),
+                rhs_scale=key_scales[4 * o:P, :],
+                start=(o == 0),
+                stop=(o == PASSES - 1),
+            )
 
         def first_tap(i, on_vector):
             acc[i] = keep.tile([P, S], F32, name=f"acc{i}")
@@ -145,48 +167,68 @@ def tile_picked_ymta_two_p_kernel(tc, x_words, x_scales, hT, gT, ka, kb, offs, o
 
         def normalise(i, on_vector):
             inv[i] = keep.tile([P, 1], F32, name=f"inv{i}")
-            nc.vector.reciprocal(out=inv[i][:], in_=total[i][:])
             result = keep.tile([P, S], F32, name=f"result{i}")
             if on_vector:
+                nc.vector.reciprocal(out=inv[i][:], in_=total[i][:])
                 nc.vector.tensor_scalar(result[:], expd[i][:], inv[i][:], None, ALU.mult)
             else:
-                nc.scalar.activation(out=result[:], in_=expd[i][:], func=ACT.Copy, scale=inv[i][:])
+                nc.gpsimd.tensor_tensor(out=inv[i][:], in0=total[i][:], in1=minus_one[:], op=ALU.pow)
+                nc.gpsimd.tensor_scalar(result[:], expd[i][:], inv[i][:], 0.0, ALU.mult, ALU.add)
             nc.sync.dma_start(out=out[i * P:(i + 1) * P, :], in_=result[:])
 
         nc.vector.tensor_copy(key_words[0][:], word_table[0][:].bitcast(U32).indirect(offsets[:]))
-        nc.vector.tensor_copy(key_words[1][:], word_table[1][:].bitcast(U32).indirect(offsets[:]))
         nc.vector.tensor_copy(key_scales[:], scale_table[:].indirect(offsets[:]))
+        nc.vector.tensor_copy(key_words[1][:], word_table[1][:].bitcast(U32).indirect(offsets[:]))
 
-        on_vector = {("h", 0, 0), ("h", 0, 1)}
+        def operands(name, first, count, o, engine):
+            cast(name, first, count, o, engine)
+            quantize(name, first, count, o)
+            for i in range(first, first + count):
+                product(name, i, o)
 
-        def operands(name, pair):
-            tiles = range(pair * PAIR, (pair + 1) * PAIR)
-            for o in range(PASSES):
-                for i in tiles:
-                    cast(name, i, o, (name, i, o) in on_vector)
-                    quantize(name, i, o)
-            for i in tiles:
-                product(name, i)
-
-        operands("h", 0)
-        for pair in range(TILES // PAIR):
-            tiles = range(pair * PAIR, (pair + 1) * PAIR)
-            for i in tiles:
-                first_tap(i, i == 0)
-            operands("g", pair)
-            for shift in (1, 2):
-                for i in tiles:
-                    add_tap("h", i, shift)
-            if pair > 0:
-                for i in tiles:
-                    normalise(i - PAIR, False)
-            if pair + 1 < TILES // PAIR:
-                operands("h", pair + 1)
-            for shift in range(TAPS):
-                for i in tiles:
-                    add_tap("g", i, shift)
-            for i in tiles:
-                row_max(i)
-                exponentiate(i)
-        for i in range(TILES - PAIR, TILES):
-            normalise(i, True)
+        operands("h", 0, 2, 0, "scalar")
+        operands("h", 0, 1, 1, "vector")
+        operands("h", 1, 1, 1, "scalar")
+        first_tap(0, True)
+        first_tap(1, False)
+        operands("g", 0, 2, 0, "scalar")
+        operands("g", 0, 1, 1, "scalar")
+        operands("g", 1, 1, 1, "scalar")
+        add_tap("h", 0, 1)
+        add_tap("h", 1, 1)
+        add_tap("h", 0, 2)
+        add_tap("h", 1, 2)
+        operands("h", 2, 2, 0, "scalar")
+        operands("h", 2, 2, 1, "scalar")
+        add_tap("g", 0, 0)
+        add_tap("g", 1, 0)
+        add_tap("g", 0, 1)
+        add_tap("g", 1, 1)
+        first_tap(2, False)
+        first_tap(3, False)
+        add_tap("g", 0, 2)
+        add_tap("g", 1, 2)
+        operands("g", 2, 2, 0, "scalar")
+        operands("g", 2, 2, 1, "scalar")
+        row_max(0)
+        exponentiate(0)
+        row_max(1)
+        exponentiate(1)
+        normalise(0, False)
+        normalise(1, False)
+        add_tap("h", 2, 1)
+        add_tap("h", 3, 1)
+        add_tap("h", 2, 2)
+        add_tap("h", 3, 2)
+        add_tap("g", 2, 0)
+        add_tap("g", 3, 0)
+        add_tap("g", 2, 1)
+        add_tap("g", 3, 1)
+        add_tap("g", 2, 2)
+        add_tap("g", 3, 2)
+        row_max(2)
+        exponentiate(2)
+        row_max(3)
+        exponentiate(3)
+        normalise(2, True)
+        normalise(3, True)

@@ -55,16 +55,16 @@ def tile_picked_ymta_two_p_kernel(tc, x_words, x_scales, hT, gT, ka, kb, offs, o
         def load_words(o):
             nc.sync.dma_start(out=word_table[o][:], in_=x_words[o].rearrange("p n t -> p (n t)").bitcast(I32))
 
-        def load_scales(o):
+        def load_scales():
             for q in range(4):
                 nc.sync.dma_start(
-                    out=scale_table[32 * q + 4 * o:32 * q + 4 * o + 4, :].bitcast(I32),
-                    in_=x_scales[o, 4 * q:4 * q + 4, :].bitcast(I32),
+                    out=scale_table[32 * q:32 * q + 4 * PASSES, :].bitcast(I32),
+                    in_=x_scales[:, 4 * q:4 * q + 4, :].bitcast(I32),
                 )
 
         def load_taps():
-            nc.sync.dma_start(out=tap_rows[0:TILES, :], in_=ka.rearrange("(i p) c -> i (p c)", p=P))
-            nc.sync.dma_start(out=tap_rows[TILES:2 * TILES, :], in_=kb.rearrange("(i p) c -> i (p c)", p=P))
+            nc.sync.dma_start(out=tap_rows[0:4 * TILES:4, :], in_=ka.rearrange("(i p) c -> i (p c)", p=P))
+            nc.sync.dma_start(out=tap_rows[4 * TILES:8 * TILES:4, :], in_=kb.rearrange("(i p) c -> i (p c)", p=P))
 
         nc.gpsimd.memset(scale_table[:].bitcast(I32), 0)
         nc.gpsimd.memset(tap_rows[:], 0.0)
@@ -75,11 +75,10 @@ def tile_picked_ymta_two_p_kernel(tc, x_words, x_scales, hT, gT, ka, kb, offs, o
         nc.scalar.activation(out=warm_out[:], in_=warm[:], func=ACT.Exp)
         load_queries("h", 0, 2, 0)
         nc.sync.dma_start(offsets[:], offs)
-        load_scales(0)
         load_words(0)
-        load_scales(1)
-        load_taps()
+        load_scales()
         load_words(1)
+        load_taps()
         load_queries("h", 0, 2, 1)
         load_queries("g", 0, 2, 0)
         load_queries("g", 0, 2, 1)
@@ -91,7 +90,7 @@ def tile_picked_ymta_two_p_kernel(tc, x_words, x_scales, hT, gT, ka, kb, offs, o
         turned = psum.tile([P, TAPS, P], F32, name="turned", tag=f"scores_g{TILES - 1}")
         for c in range(TAPS):
             nc.tensor.transpose(turned[:, c, :], tap_rows[:, c::TAPS], identity[:])
-        nc.scalar.copy(out=taps[:], in_=turned[:, :, 0:2 * TILES])
+        nc.scalar.copy(out=taps[:], in_=turned[:, :, 0:8 * TILES:4])
 
         def tap(name, i, shift):
             col = i if name == "h" else TILES + i
@@ -99,8 +98,8 @@ def tile_picked_ymta_two_p_kernel(tc, x_words, x_scales, hT, gT, ka, kb, offs, o
 
         grouped, codes, scales, scores, acc, neg_max, expd, total, inv = {}, {}, {}, {}, {}, {}, {}, {}, {}
 
-        def cast(name, first, count, o, engine):
-            tile = keep.tile([P, count * P, PACK], BF16, name=f"grouped_{name}{first}_{o}", align_bytes=64)
+        def cast(name, first, count, o, engine, slot):
+            tile = keep.tile([P, count * P, PACK], BF16, name=f"grouped_{name}{first}_{o}", tag=slot, align_bytes=64)
             loaded, at = raw[name, first, o]
             rows = loaded[:, :, at:at + count * P]
             if engine == "gpsimd":
@@ -180,26 +179,26 @@ def tile_picked_ymta_two_p_kernel(tc, x_words, x_scales, hT, gT, ka, kb, offs, o
         nc.vector.tensor_copy(key_scales[:], scale_table[:].indirect(offsets[:]))
         nc.vector.tensor_copy(key_words[1][:], word_table[1][:].bitcast(U32).indirect(offsets[:]))
 
-        def operands(name, first, count, o, engine):
-            cast(name, first, count, o, engine)
+        def operands(name, first, count, o, engine, slot):
+            cast(name, first, count, o, engine, slot)
             quantize(name, first, count, o)
             for i in range(first, first + count):
                 product(name, i, o)
 
-        operands("h", 0, 2, 0, "scalar")
-        operands("h", 0, 1, 1, "vector")
-        operands("h", 1, 1, 1, "scalar")
+        operands("h", 0, 2, 0, "scalar", "h02_0")
+        operands("h", 0, 1, 1, "vector", "h01_1")
+        operands("h", 1, 1, 1, "scalar", "h11_1")
         first_tap(0, True)
         first_tap(1, False)
-        operands("g", 0, 2, 0, "scalar")
-        operands("g", 0, 1, 1, "scalar")
-        operands("g", 1, 1, 1, "scalar")
+        operands("g", 0, 2, 0, "scalar", "g02_0")
+        operands("g", 0, 1, 1, "scalar", "g01_1")
+        operands("g", 1, 1, 1, "scalar", "g11_1")
         add_tap("h", 0, 1)
         add_tap("h", 1, 1)
         add_tap("h", 0, 2)
         add_tap("h", 1, 2)
-        operands("h", 2, 2, 0, "scalar")
-        operands("h", 2, 2, 1, "scalar")
+        operands("h", 2, 2, 0, "scalar", "h22_0")
+        operands("h", 2, 2, 1, "scalar", "h22_1")
         add_tap("g", 0, 0)
         add_tap("g", 1, 0)
         add_tap("g", 0, 1)
@@ -208,8 +207,8 @@ def tile_picked_ymta_two_p_kernel(tc, x_words, x_scales, hT, gT, ka, kb, offs, o
         first_tap(3, False)
         add_tap("g", 0, 2)
         add_tap("g", 1, 2)
-        operands("g", 2, 2, 0, "scalar")
-        operands("g", 2, 2, 1, "scalar")
+        operands("g", 2, 2, 0, "scalar", "g22_0")
+        operands("g", 2, 2, 1, "scalar", "g22_1")
         row_max(0)
         exponentiate(0)
         row_max(1)

@@ -66,8 +66,9 @@ def tile_picked_ymta_two_p_kernel(tc, x_words, x_scales, hT, gT, ka, kb, offs, o
             nc.sync.dma_start(out=tap_rows[0:4 * TILES:4, :], in_=ka.rearrange("(i p) c -> i (p c)", p=P))
             nc.sync.dma_start(out=tap_rows[4 * TILES:8 * TILES:4, :], in_=kb.rearrange("(i p) c -> i (p c)", p=P))
 
-        nc.gpsimd.memset(scale_table[:].bitcast(I32), 0)
         nc.gpsimd.memset(tap_rows[:], 0.0)
+        nc.vector.memset(scale_table[:, 0:T // 2].bitcast(I32), 0)
+        nc.gpsimd.memset(scale_table[:, T // 2:T].bitcast(I32), 0)
         nc.vector.memset(warm[:], 0.0)
         minus_one = keep.tile([P, 1], F32, name="minus_one")
         nc.gpsimd.memset(minus_one[:], -1.0)
@@ -75,10 +76,10 @@ def tile_picked_ymta_two_p_kernel(tc, x_words, x_scales, hT, gT, ka, kb, offs, o
         nc.scalar.activation(out=warm_out[:], in_=warm[:], func=ACT.Exp)
         load_queries("h", 0, 2, 0)
         nc.sync.dma_start(offsets[:], offs)
+        load_taps()
         load_words(0)
         load_scales()
         load_words(1)
-        load_taps()
         load_queries("h", 0, 2, 1)
         load_queries("g", 0, 2, 0)
         load_queries("g", 0, 2, 1)
@@ -96,6 +97,7 @@ def tile_picked_ymta_two_p_kernel(tc, x_words, x_scales, hT, gT, ka, kb, offs, o
             col = i if name == "h" else TILES + i
             return taps[:, shift, col:col + 1]
 
+        side = {}
         grouped, codes, scales, scores, acc, neg_max, expd, total, inv = {}, {}, {}, {}, {}, {}, {}, {}, {}
 
         def cast(name, first, count, o, engine, slot):
@@ -138,22 +140,35 @@ def tile_picked_ymta_two_p_kernel(tc, x_words, x_scales, hT, gT, ka, kb, offs, o
                 stop=(o == PASSES - 1),
             )
 
-        def first_tap(i, on_vector):
-            acc[i] = keep.tile([P, S], F32, name=f"acc{i}")
+        def first_tap(i, on_vector, slot, parts=1):
+            acc[i] = keep.tile([P, S], F32, name=f"acc{i}", tag=slot, align_bytes=64)
             if on_vector:
-                nc.vector.tensor_scalar(acc[i][:], scores["h", i][:], tap("h", i, 0), None, ALU.mult)
+                for at in range(0, S, S // parts):
+                    cols = slice(at, at + S // parts)
+                    nc.vector.tensor_scalar(acc[i][:, cols], scores["h", i][:, cols], tap("h", i, 0), None, ALU.mult)
             else:
                 nc.scalar.activation(out=acc[i][:], in_=scores["h", i][:], func=ACT.Copy, scale=tap("h", i, 0))
 
-        def add_tap(name, i, shift):
-            nc.vector.scalar_tensor_tensor(
-                out=acc[i][:, shift:S],
-                in0=scores[name, i][:, 0:S - shift],
-                scalar=tap(name, i, shift),
-                in1=acc[i][:, shift:S],
-                op0=ALU.mult,
-                op1=ALU.add,
+        def add_tap(name, i, shift, parts=1):
+            for at in range(0, S, S // parts):
+                lo, hi = max(at, shift), at + S // parts
+                nc.vector.scalar_tensor_tensor(
+                    out=acc[i][:, lo:hi],
+                    in0=scores[name, i][:, lo - shift:hi - shift],
+                    scalar=tap(name, i, shift),
+                    in1=acc[i][:, lo:hi],
+                    op0=ALU.mult,
+                    op1=ALU.add,
+                )
+
+        def side_tap(name, i, shift, slot):
+            side[name, i] = keep.tile([P, S - shift], F32, name=f"side_{name}{i}", tag=slot, align_bytes=64)
+            nc.scalar.activation(
+                out=side[name, i][:], in_=scores[name, i][:, 0:S - shift], func=ACT.Copy, scale=tap(name, i, shift)
             )
+
+        def add_side(name, i, shift):
+            nc.gpsimd.tensor_tensor(out=acc[i][:, shift:S], in0=acc[i][:, shift:S], in1=side[name, i][:], op=ALU.add)
 
         def row_max(i):
             neg_max[i] = keep.tile([P, 1], F32, name=f"neg_max{i}")
@@ -164,15 +179,18 @@ def tile_picked_ymta_two_p_kernel(tc, x_words, x_scales, hT, gT, ka, kb, offs, o
             total[i] = keep.tile([P, 1], F32, name=f"total{i}")
             nc.scalar.activation(out=expd[i][:], in_=acc[i][:], func=ACT.Exp, bias=neg_max[i][:], accum_out=total[i][:])
 
-        def normalise(i, on_vector):
+        def normalise(i, engine):
             inv[i] = keep.tile([P, 1], F32, name=f"inv{i}")
             result = keep.tile([P, S], F32, name=f"result{i}")
-            if on_vector:
+            if engine == "vector":
                 nc.vector.reciprocal(out=inv[i][:], in_=total[i][:])
                 nc.vector.tensor_scalar(result[:], expd[i][:], inv[i][:], None, ALU.mult)
             else:
                 nc.gpsimd.tensor_tensor(out=inv[i][:], in0=total[i][:], in1=minus_one[:], op=ALU.pow)
-                nc.gpsimd.tensor_scalar(result[:], expd[i][:], inv[i][:], 0.0, ALU.mult, ALU.add)
+                if engine == "scalar":
+                    nc.scalar.activation(out=result[:], in_=expd[i][:], func=ACT.Copy, scale=inv[i][:])
+                else:
+                    nc.gpsimd.tensor_scalar(result[:], expd[i][:], inv[i][:], 0.0, ALU.mult, ALU.add)
             nc.sync.dma_start(out=out[i * P:(i + 1) * P, :], in_=result[:])
 
         nc.vector.tensor_copy(key_words[0][:], word_table[0][:].bitcast(U32).indirect(offsets[:]))
@@ -188,46 +206,48 @@ def tile_picked_ymta_two_p_kernel(tc, x_words, x_scales, hT, gT, ka, kb, offs, o
         operands("h", 0, 2, 0, "scalar", "h02_0")
         operands("h", 0, 1, 1, "vector", "h01_1")
         operands("h", 1, 1, 1, "scalar", "h11_1")
-        first_tap(0, True)
-        first_tap(1, False)
-        operands("g", 0, 2, 0, "scalar", "g02_0")
+        operands("g", 0, 2, 0, "scalar", "a")
+        first_tap(0, True, "a")
         operands("g", 0, 1, 1, "scalar", "g01_1")
-        operands("g", 1, 1, 1, "scalar", "g11_1")
+        operands("g", 1, 1, 1, "scalar", "b")
+        first_tap(1, False, "acc1")
+        operands("h", 2, 2, 0, "gpsimd", "b")
+        operands("h", 2, 2, 1, "scalar", "h22_1")
+        operands("g", 2, 2, 0, "scalar", "g22_0")
+        operands("g", 2, 2, 1, "scalar", "d")
+        first_tap(2, False, "acc2")
+        first_tap(3, False, "acc3")
         add_tap("h", 0, 1)
         add_tap("h", 1, 1)
         add_tap("h", 0, 2)
         add_tap("h", 1, 2)
-        operands("h", 2, 2, 0, "scalar", "h22_0")
-        operands("h", 2, 2, 1, "scalar", "h22_1")
-        add_tap("g", 0, 0)
-        add_tap("g", 1, 0)
         add_tap("g", 0, 1)
         add_tap("g", 1, 1)
-        first_tap(2, False)
-        first_tap(3, False)
         add_tap("g", 0, 2)
         add_tap("g", 1, 2)
-        operands("g", 2, 2, 0, "scalar", "g22_0")
-        operands("g", 2, 2, 1, "scalar", "g22_1")
-        row_max(0)
-        exponentiate(0)
-        row_max(1)
-        exponentiate(1)
-        normalise(0, False)
-        normalise(1, False)
+        side_tap("g", 0, 0, "d")
+        side_tap("g", 1, 0, "side_g1")
+        add_side("g", 0, 0)
+        add_side("g", 1, 0)
         add_tap("h", 2, 1)
         add_tap("h", 3, 1)
         add_tap("h", 2, 2)
         add_tap("h", 3, 2)
         add_tap("g", 2, 0)
         add_tap("g", 3, 0)
+        row_max(0)
+        exponentiate(0)
         add_tap("g", 2, 1)
         add_tap("g", 3, 1)
+        row_max(1)
+        exponentiate(1)
         add_tap("g", 2, 2)
         add_tap("g", 3, 2)
         row_max(2)
         exponentiate(2)
         row_max(3)
         exponentiate(3)
-        normalise(2, True)
-        normalise(3, True)
+        normalise(0, "gpsimd")
+        normalise(1, "gpsimd")
+        normalise(2, "vector")
+        normalise(3, "vector")

@@ -209,9 +209,9 @@ def tile_picked_ymta_two_p_kernel(tc, x_words, x_scales, hT, gT, ka, kb, offs, o
         operands("g", 0, 2, 0, "scalar", "a")
         first_tap(0, True, "a")
         operands("g", 0, 1, 1, "scalar", "g01_1")
-        operands("g", 1, 1, 1, "scalar", "b")
+        operands("g", 1, 1, 1, "scalar", "g11_1")
         first_tap(1, False, "acc1")
-        operands("h", 2, 2, 0, "gpsimd", "b")
+        operands("h", 2, 2, 0, "scalar", "h22_0")
         operands("h", 2, 2, 1, "scalar", "h22_1")
         operands("g", 2, 2, 0, "scalar", "g22_0")
         operands("g", 2, 2, 1, "scalar", "d")

@@ -46,7 +46,7 @@ def tile_picked_ymta_two_p_kernel(tc, x_words, x_scales, hT, gT, ka, kb, offs, o
 
         def load_queries(name, first, count, o):
             src = hT if name == "h" else gT
-            tile = keep.tile([P, PACK, count * P], F32, name=f"raw_{name}{first}_{o}")
+            tile = keep.tile([P, PACK, count * P], F32, name=f"raw_{name}{first}_{o}", align_bytes=64)
             rows = src[o * K_PASS:(o + 1) * K_PASS, first * P:(first + count) * P]
             nc.sync.dma_start(out=tile[:], in_=rows.rearrange("(p j) w -> p j w", j=PACK))
             for m in range(count):
@@ -70,8 +70,6 @@ def tile_picked_ymta_two_p_kernel(tc, x_words, x_scales, hT, gT, ka, kb, offs, o
         nc.vector.memset(scale_table[:, 0:T // 2].bitcast(I32), 0)
         nc.gpsimd.memset(scale_table[:, T // 2:T].bitcast(I32), 0)
         nc.vector.memset(warm[:], 0.0)
-        minus_one = keep.tile([P, 1], F32, name="minus_one")
-        nc.gpsimd.memset(minus_one[:], -1.0)
         make_identity(nc, identity[:])
         nc.scalar.activation(out=warm_out[:], in_=warm[:], func=ACT.Exp)
         load_queries("h", 0, 2, 0)
@@ -88,10 +86,11 @@ def tile_picked_ymta_two_p_kernel(tc, x_words, x_scales, hT, gT, ka, kb, offs, o
         load_queries("g", 2, 2, 0)
         load_queries("g", 2, 2, 1)
 
-        turned = psum.tile([P, TAPS, P], F32, name="turned", tag=f"scores_g{TILES - 1}")
-        for c in range(TAPS):
-            nc.tensor.transpose(turned[:, c, :], tap_rows[:, c::TAPS], identity[:])
-        nc.scalar.copy(out=taps[:], in_=turned[:, :, 0:8 * TILES:4])
+        def turn_taps():
+            turned = psum.tile([P, TAPS, P], F32, name="turned", tag=f"scores_g{TILES - 1}")
+            for c in range(TAPS):
+                nc.tensor.transpose(turned[:, c, :], tap_rows[:, c::TAPS], identity[:])
+            nc.scalar.copy(out=taps[:], in_=turned[:, :, 0:8 * TILES:4])
 
         def tap(name, i, shift):
             col = i if name == "h" else TILES + i
@@ -182,49 +181,75 @@ def tile_picked_ymta_two_p_kernel(tc, x_words, x_scales, hT, gT, ka, kb, offs, o
         def normalise(i, engine):
             inv[i] = keep.tile([P, 1], F32, name=f"inv{i}")
             result = keep.tile([P, S], F32, name=f"result{i}")
+            nc.vector.reciprocal(out=inv[i][:], in_=total[i][:])
             if engine == "vector":
-                nc.vector.reciprocal(out=inv[i][:], in_=total[i][:])
                 nc.vector.tensor_scalar(result[:], expd[i][:], inv[i][:], None, ALU.mult)
             else:
-                nc.gpsimd.tensor_tensor(out=inv[i][:], in0=total[i][:], in1=minus_one[:], op=ALU.pow)
-                if engine == "scalar":
-                    nc.scalar.activation(out=result[:], in_=expd[i][:], func=ACT.Copy, scale=inv[i][:])
-                else:
-                    nc.gpsimd.tensor_scalar(result[:], expd[i][:], inv[i][:], 0.0, ALU.mult, ALU.add)
+                nc.scalar.activation(out=result[:], in_=expd[i][:], func=ACT.Copy, scale=inv[i][:])
             nc.sync.dma_start(out=out[i * P:(i + 1) * P, :], in_=result[:])
 
-        nc.vector.tensor_copy(key_words[0][:], word_table[0][:].bitcast(U32).indirect(offsets[:]))
-        nc.vector.tensor_copy(key_scales[:], scale_table[:].indirect(offsets[:]))
-        nc.vector.tensor_copy(key_words[1][:], word_table[1][:].bitcast(U32).indirect(offsets[:]))
+        def gather_words(o, parts):
+            for part in range(parts):
+                nc.vector.tensor_copy(
+                    key_words[o][:, part * S // parts:(part + 1) * S // parts],
+                    word_table[o][:].bitcast(U32).indirect(
+                        offsets[:, part * S // parts // 16:(part + 1) * S // parts // 16]
+                    ),
+                )
 
-        def operands(name, first, count, o, engine, slot):
-            cast(name, first, count, o, engine, slot)
-            quantize(name, first, count, o)
+        def gather_scales():
+            nc.vector.tensor_copy(key_scales[:], scale_table[:].indirect(offsets[:]))
+
+        def multiply(name, first, count, o):
             for i in range(first, first + count):
                 product(name, i, o)
 
-        operands("h", 0, 2, 0, "scalar", "h02_0")
-        operands("h", 0, 1, 1, "vector", "h01_1")
-        operands("h", 1, 1, 1, "scalar", "h11_1")
-        operands("g", 0, 2, 0, "scalar", "a")
-        first_tap(0, True, "a")
-        operands("g", 0, 1, 1, "scalar", "g01_1")
-        operands("g", 1, 1, 1, "scalar", "g11_1")
+        turn_taps()
+        cast("h", 0, 2, 0, "scalar", "grouped_h0_0")
+        quantize("h", 0, 2, 0)
+        gather_words(0, 1)
+        gather_scales()
+        multiply("h", 0, 2, 0)
+        gather_words(1, 1)
+        cast("h", 0, 1, 1, "vector", "grouped_h0_1")
+        cast("h", 1, 1, 1, "scalar", "grouped_h1_1")
+        quantize("h", 0, 1, 1)
+        multiply("h", 0, 1, 1)
+        quantize("h", 1, 1, 1)
+        multiply("h", 1, 1, 1)
+        cast("g", 0, 2, 0, "scalar", "grouped_g0_0")
+        cast("g", 0, 1, 1, "scalar", "grouped_g0_1")
+        first_tap(0, True, "raw_g0_0")
         first_tap(1, False, "acc1")
-        operands("h", 2, 2, 0, "scalar", "h22_0")
-        operands("h", 2, 2, 1, "scalar", "h22_1")
-        operands("g", 2, 2, 0, "scalar", "g22_0")
-        operands("g", 2, 2, 1, "scalar", "d")
-        first_tap(2, False, "acc2")
-        first_tap(3, False, "acc3")
+        cast("g", 1, 1, 1, "scalar", "grouped_g1_1")
+        quantize("g", 0, 2, 0)
+        multiply("g", 0, 2, 0)
+        cast("h", 2, 2, 0, "scalar", "grouped_h2_0")
+        cast("h", 2, 2, 1, "scalar", "grouped_h2_1")
+        cast("g", 2, 2, 0, "scalar", "grouped_g2_0")
+        cast("g", 2, 2, 1, "scalar", "d")
         add_tap("h", 0, 1)
+        quantize("g", 0, 1, 1)
+        multiply("g", 0, 1, 1)
         add_tap("h", 1, 1)
         add_tap("h", 0, 2)
+        quantize("g", 1, 1, 1)
+        multiply("g", 1, 1, 1)
         add_tap("h", 1, 2)
+        quantize("h", 2, 2, 0)
+        multiply("h", 2, 2, 0)
         add_tap("g", 0, 1)
+        quantize("h", 2, 2, 1)
+        multiply("h", 2, 2, 1)
+        first_tap(2, False, "acc2")
+        first_tap(3, False, "acc3")
         add_tap("g", 1, 1)
         add_tap("g", 0, 2)
+        quantize("g", 2, 2, 0)
+        multiply("g", 2, 2, 0)
         add_tap("g", 1, 2)
+        quantize("g", 2, 2, 1)
+        multiply("g", 2, 2, 1)
         side_tap("g", 0, 0, "d")
         side_tap("g", 1, 0, "side_g1")
         add_side("g", 0, 0)
@@ -235,19 +260,19 @@ def tile_picked_ymta_two_p_kernel(tc, x_words, x_scales, hT, gT, ka, kb, offs, o
         add_tap("h", 3, 2)
         add_tap("g", 2, 0)
         add_tap("g", 3, 0)
+        add_tap("g", 2, 1)
         row_max(0)
         exponentiate(0)
-        add_tap("g", 2, 1)
         add_tap("g", 3, 1)
         row_max(1)
         exponentiate(1)
         add_tap("g", 2, 2)
+        normalise(0, "scalar")
         add_tap("g", 3, 2)
         row_max(2)
         exponentiate(2)
         row_max(3)
         exponentiate(3)
-        normalise(0, "gpsimd")
-        normalise(1, "gpsimd")
+        normalise(1, "vector")
         normalise(2, "vector")
         normalise(3, "vector")

@@ -72,12 +72,12 @@ def tile_picked_ymta_two_p_kernel(tc, x_words, x_scales, hT, gT, ka, kb, offs, o
         nc.vector.memset(warm[:], 0.0)
         make_identity(nc, identity[:])
         nc.scalar.activation(out=warm_out[:], in_=warm[:], func=ACT.Exp)
-        load_queries("h", 0, 2, 0)
         nc.sync.dma_start(offsets[:], offs)
-        load_taps()
         load_words(0)
+        load_taps()
         load_scales()
         load_words(1)
+        load_queries("h", 0, 2, 0)
         load_queries("h", 0, 2, 1)
         load_queries("g", 0, 2, 0)
         load_queries("g", 0, 2, 1)
@@ -205,12 +205,15 @@ def tile_picked_ymta_two_p_kernel(tc, x_words, x_scales, hT, gT, ka, kb, offs, o
                 product(name, i, o)
 
         turn_taps()
-        cast("h", 0, 2, 0, "scalar", "grouped_h0_0")
-        quantize("h", 0, 2, 0)
         gather_words(0, 1)
         gather_scales()
-        multiply("h", 0, 2, 0)
         gather_words(1, 1)
+        cast("h", 0, 1, 0, "vector", "grouped_h0_0")
+        cast("h", 1, 1, 0, "scalar", "grouped_h1_0")
+        quantize("h", 0, 1, 0)
+        multiply("h", 0, 1, 0)
+        quantize("h", 1, 1, 0)
+        multiply("h", 1, 1, 0)
         cast("h", 0, 1, 1, "vector", "grouped_h0_1")
         cast("h", 1, 1, 1, "scalar", "grouped_h1_1")
         quantize("h", 0, 1, 1)

@@ -70,6 +70,8 @@ def tile_picked_ymta_two_p_kernel(tc, x_words, x_scales, hT, gT, ka, kb, offs, o
         nc.vector.memset(scale_table[:, 0:T // 2].bitcast(I32), 0)
         nc.gpsimd.memset(scale_table[:, T // 2:T].bitcast(I32), 0)
         nc.vector.memset(warm[:], 0.0)
+        minus_one = keep.tile([P, 1], F32, name="minus_one")
+        nc.gpsimd.memset(minus_one[:], -1.0)
         make_identity(nc, identity[:])
         nc.scalar.activation(out=warm_out[:], in_=warm[:], func=ACT.Exp)
         nc.sync.dma_start(offsets[:], offs)
@@ -181,11 +183,15 @@ def tile_picked_ymta_two_p_kernel(tc, x_words, x_scales, hT, gT, ka, kb, offs, o
         def normalise(i, engine):
             inv[i] = keep.tile([P, 1], F32, name=f"inv{i}")
             result = keep.tile([P, S], F32, name=f"result{i}")
-            nc.vector.reciprocal(out=inv[i][:], in_=total[i][:])
             if engine == "vector":
+                nc.vector.reciprocal(out=inv[i][:], in_=total[i][:])
                 nc.vector.tensor_scalar(result[:], expd[i][:], inv[i][:], None, ALU.mult)
             else:
-                nc.scalar.activation(out=result[:], in_=expd[i][:], func=ACT.Copy, scale=inv[i][:])
+                nc.gpsimd.tensor_tensor(out=inv[i][:], in0=total[i][:], in1=minus_one[:], op=ALU.pow)
+                if engine == "scalar":
+                    nc.scalar.activation(out=result[:], in_=expd[i][:], func=ACT.Copy, scale=inv[i][:])
+                else:
+                    nc.gpsimd.tensor_scalar(result[:], expd[i][:], inv[i][:], 0.0, ALU.mult, ALU.add)
             nc.sync.dma_start(out=out[i * P:(i + 1) * P, :], in_=result[:])
 
         def gather_words(o, parts):
@@ -254,6 +260,7 @@ def tile_picked_ymta_two_p_kernel(tc, x_words, x_scales, hT, gT, ka, kb, offs, o
         quantize("g", 2, 2, 1)
         multiply("g", 2, 2, 1)
         side_tap("g", 0, 0, "d")
+        side_tap("g", 2, 0, "side_g2")
         side_tap("g", 1, 0, "side_g1")
         add_side("g", 0, 0)
         add_side("g", 1, 0)
@@ -261,21 +268,21 @@ def tile_picked_ymta_two_p_kernel(tc, x_words, x_scales, hT, gT, ka, kb, offs, o
         add_tap("h", 3, 1)
         add_tap("h", 2, 2)
         add_tap("h", 3, 2)
-        add_tap("g", 2, 0)
-        add_tap("g", 3, 0)
         add_tap("g", 2, 1)
+        add_tap("g", 3, 0)
+        add_tap("g", 2, 2)
+        add_side("g", 2, 0)
+        add_tap("g", 3, 1)
         row_max(0)
         exponentiate(0)
-        add_tap("g", 3, 1)
+        add_tap("g", 3, 2)
         row_max(1)
         exponentiate(1)
-        add_tap("g", 2, 2)
-        normalise(0, "scalar")
-        add_tap("g", 3, 2)
-        row_max(2)
-        exponentiate(2)
         row_max(3)
         exponentiate(3)
+        row_max(2)
+        exponentiate(2)
+        normalise(0, "gpsimd")
         normalise(1, "vector")
-        normalise(2, "vector")
         normalise(3, "vector")
+        normalise(2, "vector")

@@ -108,8 +108,8 @@ def tile_picked_ymta_two_p_kernel(tc, x_words, x_scales, hT, gT, ka, kb, offs, o
             if engine == "gpsimd":
                 nc.gpsimd.tensor_scalar(tile[:], rows.rearrange("p t w -> p w t"), 1.0, 0.0, ALU.mult, ALU.add)
             else:
-                dst = tile[:].rearrange("p (c i) t -> p c t i", i=4)
-                src = rows.rearrange("p t (c i) -> p c t i", i=4)
+                dst = tile[:].rearrange("p (c i) t -> p c t i", i=2)
+                src = rows.rearrange("p t (c i) -> p c t i", i=2)
                 if engine == "vector":
                     nc.vector.tensor_copy(out=dst, in_=src)
                 else:

@@ -20,8 +20,9 @@ PACK = 4
 K_PASS = P * PACK
 PASSES = K // K_PASS
 TILES = V // P
-PAIR = 2
 TAPS = 3
+RUN = 2
+ROW = 4 * S
 FLOPS = 2 * 2 * K * S * V
 
 
@@ -31,9 +32,25 @@ def tile_picked_ymta_two_p_kernel(tc, x_words, x_scales, hT, gT, ka, kb, offs, o
         keep = ctx.enter_context(tc.tile_pool(name="keep", bufs=1))
         psum = ctx.enter_context(tc.psum_pool(name="psum", bufs=1))
 
+        work = ctx.enter_context(tc.tile_pool(name="work", bufs=1))
+        start_of = {}
+        free_from = [0]
+
+        def place(shape, dtype, width, name, over=None):
+            if over is None:
+                start_of[name] = free_from[0]
+                free_from[0] = free_from[0] + width
+            else:
+                start_of[name] = start_of[over[0]] + over[1]
+            return work.tile(shape, dtype, name=name, offset=start_of[name], align_bytes=64)
+
+        def reserve(name, width):
+            start_of[name] = free_from[0]
+            free_from[0] = free_from[0] + width
+
         offsets = keep.tile([P, S // 16], U16, name="offsets")
-        word_table = [keep.tile([P, T], I32, name=f"word_table{o}", align_bytes=64) for o in range(PASSES)]
-        scale_table = keep.tile([P, T], U8, name="scale_table", align_bytes=64)
+        word_table = [place([P, T], I32, 4 * T, f"word_table{o}") for o in range(PASSES)]
+        scale_table = place([P, T], U8, T, "scale_table")
         key_words = [keep.tile([P, S], U32, name=f"key_words{o}", align_bytes=64) for o in range(PASSES)]
         key_scales = keep.tile([P, S], U8, name="key_scales", align_bytes=64)
         tap_rows = keep.tile([P, P * TAPS], F32, name="tap_rows")
@@ -42,11 +59,15 @@ def tile_picked_ymta_two_p_kernel(tc, x_words, x_scales, hT, gT, ka, kb, offs, o
         warm = keep.tile([P, 8], F32, name="warm")
         warm_out = keep.tile([P, 8], F32, name="warm_out")
 
-        raw = {}
+        raw, grouped, codes, scales, scores, acc, side = {}, {}, {}, {}, {}, {}, {}
+        rounded, neg_max, expd, total, inv = {}, {}, {}, {}, {}
+
+        def load_list():
+            nc.sync.dma_start(offsets[:], offs)
 
         def load_queries(name, first, count, o):
             src = hT if name == "h" else gT
-            tile = keep.tile([P, PACK, count * P], F32, name=f"raw_{name}{first}_{o}", align_bytes=64)
+            tile = place([P, PACK, count * P], F32, 4 * PACK * count * P, f"raw_{name}{first}_{o}")
             rows = src[o * K_PASS:(o + 1) * K_PASS, first * P:(first + count) * P]
             nc.sync.dma_start(out=tile[:], in_=rows.rearrange("(p j) w -> p j w", j=PACK))
             for m in range(count):
@@ -55,9 +76,9 @@ def tile_picked_ymta_two_p_kernel(tc, x_words, x_scales, hT, gT, ka, kb, offs, o
         def load_words(o):
             nc.sync.dma_start(out=word_table[o][:], in_=x_words[o].rearrange("p n t -> p (n t)").bitcast(I32))
 
-        def load_scales():
+        def load_scales(queue):
             for q in range(4):
-                nc.sync.dma_start(
+                queue.dma_start(
                     out=scale_table[32 * q:32 * q + 4 * PASSES, :].bitcast(I32),
                     in_=x_scales[:, 4 * q:4 * q + 4, :].bitcast(I32),
                 )
@@ -66,30 +87,8 @@ def tile_picked_ymta_two_p_kernel(tc, x_words, x_scales, hT, gT, ka, kb, offs, o
             nc.sync.dma_start(out=tap_rows[0:4 * TILES:4, :], in_=ka.rearrange("(i p) c -> i (p c)", p=P))
             nc.sync.dma_start(out=tap_rows[4 * TILES:8 * TILES:4, :], in_=kb.rearrange("(i p) c -> i (p c)", p=P))
 
-        nc.gpsimd.memset(tap_rows[:], 0.0)
-        nc.vector.memset(scale_table[:, 0:T // 2].bitcast(I32), 0)
-        nc.gpsimd.memset(scale_table[:, T // 2:T].bitcast(I32), 0)
-        nc.vector.memset(warm[:], 0.0)
-        minus_one = keep.tile([P, 1], F32, name="minus_one")
-        nc.gpsimd.memset(minus_one[:], -1.0)
-        make_identity(nc, identity[:])
-        nc.scalar.activation(out=warm_out[:], in_=warm[:], func=ACT.Exp)
-        nc.sync.dma_start(offsets[:], offs)
-        load_words(0)
-        load_taps()
-        load_scales()
-        load_words(1)
-        load_queries("h", 0, 2, 0)
-        load_queries("h", 0, 2, 1)
-        load_queries("g", 0, 2, 0)
-        load_queries("g", 0, 2, 1)
-        load_queries("h", 2, 2, 0)
-        load_queries("h", 2, 2, 1)
-        load_queries("g", 2, 2, 0)
-        load_queries("g", 2, 2, 1)
-
-        def turn_taps():
-            turned = psum.tile([P, TAPS, P], F32, name="turned", tag=f"scores_g{TILES - 1}")
+        def turn_taps(bank):
+            turned = psum.tile([P, TAPS, P], F32, name="turned", tag=bank)
             for c in range(TAPS):
                 nc.tensor.transpose(turned[:, c, :], tap_rows[:, c::TAPS], identity[:])
             nc.scalar.copy(out=taps[:], in_=turned[:, :, 0:8 * TILES:4])
@@ -98,37 +97,34 @@ def tile_picked_ymta_two_p_kernel(tc, x_words, x_scales, hT, gT, ka, kb, offs, o
             col = i if name == "h" else TILES + i
             return taps[:, shift, col:col + 1]
 
-        side = {}
-        grouped, codes, scales, scores, acc, neg_max, expd, total, inv = {}, {}, {}, {}, {}, {}, {}, {}, {}
-
-        def cast(name, first, count, o, engine, slot):
-            tile = keep.tile([P, count * P, PACK], BF16, name=f"grouped_{name}{first}_{o}", tag=slot, align_bytes=64)
+        def cast(name, first, count, o, engine, over=None):
+            tile = place([P, count * P, PACK], BF16, ROW, f"grouped_{name}{first}_{o}", over)
             loaded, at = raw[name, first, o]
             rows = loaded[:, :, at:at + count * P]
-            if engine == "gpsimd":
+            dst = tile[:].rearrange("p (c i) t -> p c t i", i=RUN)
+            src = rows.rearrange("p t (c i) -> p c t i", i=RUN)
+            if engine == "vector":
+                nc.vector.tensor_copy(out=dst, in_=src)
+            elif engine == "gpsimd":
                 nc.gpsimd.tensor_scalar(tile[:], rows.rearrange("p t w -> p w t"), 1.0, 0.0, ALU.mult, ALU.add)
             else:
-                dst = tile[:].rearrange("p (c i) t -> p c t i", i=2)
-                src = rows.rearrange("p t (c i) -> p c t i", i=2)
-                if engine == "vector":
-                    nc.vector.tensor_copy(out=dst, in_=src)
-                else:
-                    nc.scalar.copy(out=dst, in_=src)
+                nc.scalar.copy(out=dst, in_=src)
             grouped[name, first, o] = tile
 
-        def quantize(name, first, count, o):
-            words = keep.tile([P, count * P], U32, name=f"codes_{name}{first}_{o}", align_bytes=64)
+        def quantize(name, first, count, o, over=None):
+            words = place([P, count * P], U32, 4 * count * P, f"codes_{name}{first}_{o}", over)
             plane = keep.tile([P, count * P], U8, name=f"scales_{name}{first}_{o}", align_bytes=64)
             nc.vector.quantize_mx(
                 out=words[:].bitcast(FP8X4),
                 scales=plane[:],
                 in_=grouped[name, first, o][:].rearrange("p w t -> p (w t)"),
             )
-            for m in range(count):
-                codes[name, first + m, o] = words[:, m * P:(m + 1) * P]
-                scales[name, first + m, o] = plane[:, m * P:(m + 1) * P]
+            for i in range(first, first + count):
+                cols = slice((i - first) * P, (i - first + 1) * P)
+                codes[name, i, o] = words[:, cols]
+                scales[name, i, o] = plane[:, cols]
 
-        def product(name, i, o):
+        def multiply(name, i, o):
             if o == 0:
                 scores[name, i] = psum.tile([P, S], F32, name=f"scores_{name}{i}", tag=f"scores_{name}{i}")
             nc.tensor.matmul_mx(
@@ -141,130 +137,170 @@ def tile_picked_ymta_two_p_kernel(tc, x_words, x_scales, hT, gT, ka, kb, offs, o
                 stop=(o == PASSES - 1),
             )
 
-        def first_tap(i, on_vector, slot, parts=1):
-            acc[i] = keep.tile([P, S], F32, name=f"acc{i}", tag=slot, align_bytes=64)
-            if on_vector:
-                for at in range(0, S, S // parts):
-                    cols = slice(at, at + S // parts)
-                    nc.vector.tensor_scalar(acc[i][:, cols], scores["h", i][:, cols], tap("h", i, 0), None, ALU.mult)
+        def first_tap(i, engine, over=None):
+            acc[i] = place([P, S], F32, ROW, f"acc{i}", over)
+            if engine == "vector":
+                nc.vector.tensor_scalar(acc[i][:], scores["h", i][:], tap("h", i, 0), None, ALU.mult)
             else:
                 nc.scalar.activation(out=acc[i][:], in_=scores["h", i][:], func=ACT.Copy, scale=tap("h", i, 0))
 
-        def add_tap(name, i, shift, parts=1):
-            for at in range(0, S, S // parts):
-                lo, hi = max(at, shift), at + S // parts
-                nc.vector.scalar_tensor_tensor(
-                    out=acc[i][:, lo:hi],
-                    in0=scores[name, i][:, lo - shift:hi - shift],
-                    scalar=tap(name, i, shift),
-                    in1=acc[i][:, lo:hi],
-                    op0=ALU.mult,
-                    op1=ALU.add,
-                )
-
-        def side_tap(name, i, shift, slot):
-            side[name, i] = keep.tile([P, S - shift], F32, name=f"side_{name}{i}", tag=slot, align_bytes=64)
-            nc.scalar.activation(
-                out=side[name, i][:], in_=scores[name, i][:, 0:S - shift], func=ACT.Copy, scale=tap(name, i, shift)
+        def add_tap(name, i, shift, over=None):
+            before = acc[i]
+            if over is not None:
+                acc[i] = place([P, S], F32, ROW, f"moved_{name}{i}", over)
+            nc.vector.scalar_tensor_tensor(
+                out=acc[i][:, shift:S],
+                in0=scores[name, i][:, 0:S - shift],
+                scalar=tap(name, i, shift),
+                in1=before[:, shift:S],
+                op0=ALU.mult,
+                op1=ALU.add,
             )
 
-        def add_side(name, i, shift):
-            nc.gpsimd.tensor_tensor(out=acc[i][:, shift:S], in0=acc[i][:, shift:S], in1=side[name, i][:], op=ALU.add)
+        def clear_side(name, i, shift):
+            side[name, i, shift] = place([P, S], F32, ROW, f"side_{name}{i}_{shift}")
+            nc.gpsimd.memset(side[name, i, shift][:, 0:shift], 0.0)
 
-        def row_max(i):
-            neg_max[i] = keep.tile([P, 1], F32, name=f"neg_max{i}")
+        def side_tap(name, i, shift, over=None):
+            if shift == 0:
+                side[name, i, shift] = place([P, S], F32, ROW, f"side_{name}{i}_{shift}", over)
+            nc.scalar.activation(
+                out=side[name, i, shift][:, shift:S],
+                in_=scores[name, i][:, 0:S - shift],
+                func=ACT.Copy,
+                scale=tap(name, i, shift),
+            )
+
+        def add_side(name, i, shift, over=None):
+            before = acc[i]
+            if over is not None:
+                acc[i] = place([P, S], F32, ROW, f"joined_{name}{i}_{shift}", over)
+            nc.gpsimd.tensor_tensor(out=acc[i][:], in0=before[:], in1=side[name, i, shift][:], op=ALU.add)
+
+        def row_max(i, over=None):
+            neg_max[i] = place([P, 1], F32, 64, f"neg_max{i}", over)
             nc.vector.tensor_reduce(out=neg_max[i][:], in_=acc[i][:], axis=AXIS.X, op=ALU.max, negate=True)
+
+        def round_scores(i):
+            rounded[i] = place([P, S], BF16, ROW, f"rounded{i}")
+            nc.scalar.copy(out=rounded[i][:], in_=acc[i][:])
+
+        def row_max_rounded(i):
+            flipped = keep.tile([P, S], BF16, name=f"flipped{i}", align_bytes=64)
+            neg_max[i] = keep.tile([P, 1], F32, name=f"neg_max{i}")
+            nc.vector.tensor_scalar(flipped[:], rounded[i][:], -1.0, None, ALU.mult, ALU.min, accum_out=neg_max[i][:])
 
         def exponentiate(i):
             expd[i] = keep.tile([P, S], F32, name=f"expd{i}")
             total[i] = keep.tile([P, 1], F32, name=f"total{i}")
             nc.scalar.activation(out=expd[i][:], in_=acc[i][:], func=ACT.Exp, bias=neg_max[i][:], accum_out=total[i][:])
 
-        def normalise(i, engine):
-            inv[i] = keep.tile([P, 1], F32, name=f"inv{i}")
-            result = keep.tile([P, S], F32, name=f"result{i}")
-            if engine == "vector":
+        def invert(i, engine, over=None):
+            inv[i] = place([P, 1], F32, 64, f"inv{i}", over)
+            if engine == "gpsimd":
+                nc.gpsimd.tensor_tensor(out=inv[i][:], in0=total[i][:], in1=minus_one[:], op=ALU.pow)
+            else:
                 nc.vector.reciprocal(out=inv[i][:], in_=total[i][:])
+
+        def scale_and_store(i, engine, over=None):
+            result = place([P, S], F32, ROW, f"result{i}", over)
+            if engine == "gpsimd":
+                nc.gpsimd.tensor_scalar(result[:], expd[i][:], inv[i][:], 0.0, ALU.mult, ALU.add)
+            elif engine == "vector":
                 nc.vector.tensor_scalar(result[:], expd[i][:], inv[i][:], None, ALU.mult)
             else:
-                nc.gpsimd.tensor_tensor(out=inv[i][:], in0=total[i][:], in1=minus_one[:], op=ALU.pow)
-                if engine == "scalar":
-                    nc.scalar.activation(out=result[:], in_=expd[i][:], func=ACT.Copy, scale=inv[i][:])
-                else:
-                    nc.gpsimd.tensor_scalar(result[:], expd[i][:], inv[i][:], 0.0, ALU.mult, ALU.add)
+                nc.scalar.activation(out=result[:], in_=expd[i][:], func=ACT.Copy, scale=inv[i][:])
             nc.sync.dma_start(out=out[i * P:(i + 1) * P, :], in_=result[:])
 
-        def gather_words(o, parts):
-            for part in range(parts):
-                nc.vector.tensor_copy(
-                    key_words[o][:, part * S // parts:(part + 1) * S // parts],
-                    word_table[o][:].bitcast(U32).indirect(
-                        offsets[:, part * S // parts // 16:(part + 1) * S // parts // 16]
-                    ),
-                )
+        def normalise(i, engine, over=None):
+            invert(i, engine, over)
+            scale_and_store(i, engine)
+
+        def gather_words(o):
+            nc.vector.tensor_copy(key_words[o][:], word_table[o][:].bitcast(U32).indirect(offsets[:]))
 
         def gather_scales():
             nc.vector.tensor_copy(key_scales[:], scale_table[:].indirect(offsets[:]))
 
-        def multiply(name, first, count, o):
-            for i in range(first, first + count):
-                product(name, i, o)
+        minus_one = keep.tile([P, 1], F32, name="minus_one")
 
-        turn_taps()
-        gather_words(0, 1)
+        nc.gpsimd.memset(tap_rows[:], 0.0)
+        nc.vector.memset(scale_table[:, 0:T // 2].bitcast(I32), 0)
+        nc.gpsimd.memset(scale_table[:, T // 2:T].bitcast(I32), 0)
+        nc.vector.memset(warm[:], 0.0)
+        nc.gpsimd.memset(minus_one[:], -1.0)
+        make_identity(nc, identity[:])
+        nc.scalar.activation(out=warm_out[:], in_=warm[:], func=ACT.Exp)
+        load_list()
+        load_queries("h", 0, 4, 0)
+        load_taps()
+        load_scales(nc.sync)
+        load_words(0)
+        load_words(1)
+        load_queries("h", 0, 2, 1)
+        load_queries("g", 0, 2, 0)
+        load_queries("g", 0, 2, 1)
+        load_queries("h", 2, 2, 1)
+        load_queries("g", 2, 2, 0)
+        load_queries("g", 2, 2, 1)
+        turn_taps("scores_g3")
         gather_scales()
-        gather_words(1, 1)
-        cast("h", 0, 1, 0, "vector", "grouped_h0_0")
-        cast("h", 1, 1, 0, "scalar", "grouped_h1_0")
-        quantize("h", 0, 1, 0)
-        multiply("h", 0, 1, 0)
-        quantize("h", 1, 1, 0)
-        multiply("h", 1, 1, 0)
-        cast("h", 0, 1, 1, "vector", "grouped_h0_1")
-        cast("h", 1, 1, 1, "scalar", "grouped_h1_1")
+        gather_words(0)
+        cast("h", 0, 2, 0, "scalar")
+        cast("h", 2, 2, 0, "scalar")
+        quantize("h", 0, 2, 0, ("scale_table", 0))
+        multiply("h", 0, 0)
+        multiply("h", 1, 0)
+        quantize("h", 2, 2, 0, ("word_table0", 0))
+        multiply("h", 2, 0)
+        multiply("h", 3, 0)
+        gather_words(1)
+        cast("h", 0, 1, 1, "vector")
+        cast("h", 1, 1, 1, "scalar")
         quantize("h", 0, 1, 1)
-        multiply("h", 0, 1, 1)
+        multiply("h", 0, 1)
         quantize("h", 1, 1, 1)
-        multiply("h", 1, 1, 1)
-        cast("g", 0, 2, 0, "scalar", "grouped_g0_0")
-        cast("g", 0, 1, 1, "scalar", "grouped_g0_1")
-        first_tap(0, True, "raw_g0_0")
-        first_tap(1, False, "acc1")
-        cast("g", 1, 1, 1, "scalar", "grouped_g1_1")
-        quantize("g", 0, 2, 0)
-        multiply("g", 0, 2, 0)
-        cast("h", 2, 2, 0, "scalar", "grouped_h2_0")
-        cast("h", 2, 2, 1, "scalar", "grouped_h2_1")
-        cast("g", 2, 2, 0, "scalar", "grouped_g2_0")
-        cast("g", 2, 2, 1, "scalar", "d")
+        multiply("h", 1, 1)
+        cast("g", 0, 2, 0, "scalar")
+        first_tap(0, "vector")
+        first_tap(1, "scalar", ("raw_g0_0", 0))
+        cast("g", 0, 1, 1, "scalar")
+        cast("g", 1, 1, 1, "scalar")
+        cast("h", 2, 2, 1, "scalar")
+        cast("g", 2, 2, 0, "scalar")
         add_tap("h", 0, 1)
-        quantize("g", 0, 1, 1)
-        multiply("g", 0, 1, 1)
-        add_tap("h", 1, 1)
+        quantize("g", 0, 2, 0)
+        multiply("g", 0, 0)
+        multiply("g", 1, 0)
         add_tap("h", 0, 2)
+        quantize("g", 0, 1, 1)
+        multiply("g", 0, 1)
+        add_tap("h", 1, 1)
         quantize("g", 1, 1, 1)
-        multiply("g", 1, 1, 1)
+        multiply("g", 1, 1)
         add_tap("h", 1, 2)
-        quantize("h", 2, 2, 0)
-        multiply("h", 2, 2, 0)
-        add_tap("g", 0, 1)
         quantize("h", 2, 2, 1)
-        multiply("h", 2, 2, 1)
-        first_tap(2, False, "acc2")
-        first_tap(3, False, "acc3")
+        multiply("h", 2, 1)
+        multiply("h", 3, 1)
+        first_tap(2, "scalar")
+        cast("g", 2, 2, 1, "scalar")
+        first_tap(3, "scalar")
+        add_tap("g", 0, 1)
         add_tap("g", 1, 1)
         add_tap("g", 0, 2)
         quantize("g", 2, 2, 0)
-        multiply("g", 2, 2, 0)
+        multiply("g", 2, 0)
+        multiply("g", 3, 0)
         add_tap("g", 1, 2)
+        add_tap("h", 2, 1)
         quantize("g", 2, 2, 1)
-        multiply("g", 2, 2, 1)
-        side_tap("g", 0, 0, "d")
-        side_tap("g", 2, 0, "side_g2")
-        side_tap("g", 1, 0, "side_g1")
+        multiply("g", 2, 1)
+        multiply("g", 3, 1)
+        side_tap("g", 0, 0, ("grouped_g2_1", 0))
+        side_tap("g", 2, 0)
+        side_tap("g", 1, 0)
         add_side("g", 0, 0)
         add_side("g", 1, 0)
-        add_tap("h", 2, 1)
         add_tap("h", 3, 1)
         add_tap("h", 2, 2)
         add_tap("h", 3, 2)
@@ -273,16 +309,18 @@ def tile_picked_ymta_two_p_kernel(tc, x_words, x_scales, hT, gT, ka, kb, offs, o
         add_tap("g", 2, 2)
         add_side("g", 2, 0)
         add_tap("g", 3, 1)
-        row_max(0)
+        round_scores(0)
+        row_max_rounded(0)
         exponentiate(0)
         add_tap("g", 3, 2)
-        row_max(1)
+        round_scores(1)
+        row_max_rounded(1)
         exponentiate(1)
         row_max(3)
         exponentiate(3)
         row_max(2)
         exponentiate(2)
-        normalise(0, "gpsimd")
+        normalise(0, "gpsimd", ("side_g2_0", 0))
         normalise(1, "vector")
         normalise(3, "vector")
         normalise(2, "vector")

@@ -111,6 +111,15 @@ def tile_picked_ymta_two_p_kernel(tc, x_words, x_scales, hT, gT, ka, kb, offs, o
                 nc.scalar.copy(out=dst, in_=src)
             grouped[name, first, o] = tile
 
+        def cast_shared(name, first, o):
+            tile = place([P, 2 * P, PACK], BF16, ROW, f"grouped_{name}{first}_{o}")
+            loaded, at = raw[name, first, o]
+            for m, copy in enumerate((nc.vector.tensor_copy, nc.scalar.copy)):
+                dst = tile[:, m * P:(m + 1) * P, :].rearrange("p (c i) t -> p c t i", i=RUN)
+                src = loaded[:, :, at + m * P:at + (m + 1) * P].rearrange("p t (c i) -> p c t i", i=RUN)
+                copy(out=dst, in_=src)
+            grouped[name, first, o] = tile
+
         def quantize(name, first, count, o, over=None):
             words = place([P, count * P], U32, 4 * count * P, f"codes_{name}{first}_{o}", over)
             plane = keep.tile([P, count * P], U8, name=f"scales_{name}{first}_{o}", align_bytes=64)
@@ -185,8 +194,8 @@ def tile_picked_ymta_two_p_kernel(tc, x_words, x_scales, hT, gT, ka, kb, offs, o
             rounded[i] = place([P, S], BF16, ROW, f"rounded{i}")
             nc.scalar.copy(out=rounded[i][:], in_=acc[i][:])
 
-        def row_max_rounded(i):
-            flipped = keep.tile([P, S], BF16, name=f"flipped{i}", align_bytes=64)
+        def row_max_rounded(i, over=None):
+            flipped = place([P, S], BF16, ROW // 2, f"flipped{i}", over)
             neg_max[i] = keep.tile([P, 1], F32, name=f"neg_max{i}")
             nc.vector.tensor_scalar(flipped[:], rounded[i][:], -1.0, None, ALU.mult, ALU.min, accum_out=neg_max[i][:])
 
@@ -232,11 +241,11 @@ def tile_picked_ymta_two_p_kernel(tc, x_words, x_scales, hT, gT, ka, kb, offs, o
         make_identity(nc, identity[:])
         nc.scalar.activation(out=warm_out[:], in_=warm[:], func=ACT.Exp)
         load_list()
-        load_queries("h", 0, 4, 0)
+        load_words(0)
         load_taps()
         load_scales(nc.sync)
-        load_words(0)
         load_words(1)
+        load_queries("h", 0, 4, 0)
         load_queries("h", 0, 2, 1)
         load_queries("g", 0, 2, 0)
         load_queries("g", 0, 2, 1)
@@ -244,23 +253,25 @@ def tile_picked_ymta_two_p_kernel(tc, x_words, x_scales, hT, gT, ka, kb, offs, o
         load_queries("g", 2, 2, 0)
         load_queries("g", 2, 2, 1)
         turn_taps("scores_g3")
-        gather_scales()
         gather_words(0)
-        cast("h", 0, 2, 0, "scalar")
-        cast("h", 2, 2, 0, "scalar")
-        quantize("h", 0, 2, 0, ("scale_table", 0))
-        multiply("h", 0, 0)
-        multiply("h", 1, 0)
-        quantize("h", 2, 2, 0, ("word_table0", 0))
-        multiply("h", 2, 0)
-        multiply("h", 3, 0)
+        gather_scales()
         gather_words(1)
+        cast("h", 0, 1, 0, "vector")
+        cast("h", 1, 1, 0, "scalar")
+        cast("h", 2, 2, 0, "scalar")
+        quantize("h", 0, 1, 0)
+        multiply("h", 0, 0)
+        quantize("h", 1, 1, 0)
+        multiply("h", 1, 0)
         cast("h", 0, 1, 1, "vector")
         cast("h", 1, 1, 1, "scalar")
         quantize("h", 0, 1, 1)
         multiply("h", 0, 1)
+        quantize("h", 2, 2, 0)
         quantize("h", 1, 1, 1)
         multiply("h", 1, 1)
+        multiply("h", 2, 0)
+        multiply("h", 3, 0)
         cast("g", 0, 2, 0, "scalar")
         first_tap(0, "vector")
         first_tap(1, "scalar", ("raw_g0_0", 0))

@@ -23,6 +23,8 @@ TILES = V // P
 TAPS = 3
 RUN = 2
 ROW = 4 * S
+PAD = 8
+NUDGE = 2.0 ** -64
 FLOPS = 2 * 2 * K * S * V
 
 
@@ -60,6 +62,11 @@ def tile_picked_ymta_two_p_kernel(tc, x_words, x_scales, hT, gT, ka, kb, offs, o
         warm_out = keep.tile([P, 8], F32, name="warm_out")
 
         raw, grouped, codes, scales, scores, acc, side = {}, {}, {}, {}, {}, {}, {}
+        term, summed, terms_left = {}, {}, {}
+        nudge = keep.tile([P, 2 * TILES], F32, name="nudge")
+        pivot = keep.tile([P, 2 * TILES], F32, name="pivot")
+        raised = keep.tile([P, 2 * TILES], F32, name="raised")
+        ratios = keep.tile([P, TAPS - 1, 2 * TILES], F32, name="ratios")
         rounded, neg_max, expd, total, inv = {}, {}, {}, {}, {}
 
         def load_list():
@@ -186,12 +193,88 @@ def tile_picked_ymta_two_p_kernel(tc, x_words, x_scales, hT, gT, ka, kb, offs, o
                 acc[i] = place([P, S], F32, ROW, f"joined_{name}{i}_{shift}", over)
             nc.gpsimd.tensor_tensor(out=acc[i][:], in0=before[:], in1=side[name, i, shift][:], op=ALU.add)
 
+        def tap_ratios(over=None):
+            nc.gpsimd.tensor_scalar(nudge[:], taps[:, 0, :], 0.0, 2.0 * NUDGE, ALU.is_ge, ALU.mult)
+            nc.gpsimd.tensor_tensor(out=raised[:], in0=nudge[:], in1=taps[:, 0, :], op=ALU.add)
+            nc.gpsimd.tensor_scalar(pivot[:], raised[:], 1.0, -NUDGE, ALU.mult, ALU.add)
+            inv_pivot = place([P, 2 * TILES], F32, 64, "inv_pivot", over)
+            nc.vector.reciprocal(out=inv_pivot[:], in_=pivot[:])
+            nc.gpsimd.tensor_tensor(
+                out=ratios[:],
+                in0=taps[:, 1:TAPS, :],
+                in1=inv_pivot[:].unsqueeze(1).to_broadcast([P, TAPS - 1, 2 * TILES]),
+                op=ALU.mult,
+            )
+
+        def column(name, i):
+            return i if name == "h" else TILES + i
+
+        def clear_pads(i):
+            for name in ("h", "g"):
+                for shift in range(1, TAPS):
+                    term[name, i, shift] = place([P, PAD + S], F32, ROW + 64, f"term_{name}{i}_{shift}")
+                    nc.gpsimd.memset(term[name, i, shift][:, 0:PAD], 0.0)
+
+        def base_term(name, i, engine="scalar", over=None):
+            term[name, i, 0] = place([P, S], F32, ROW, f"term_{name}{i}_0", over)
+            col = column(name, i)
+            if engine == "vector":
+                nc.vector.tensor_scalar(term[name, i, 0][:], scores[name, i][:], pivot[:, col:col + 1], None, ALU.mult)
+            else:
+                nc.scalar.activation(out=term[name, i, 0][:], in_=scores[name, i][:], func=ACT.Copy, scale=pivot[:, col:col + 1])
+
+        def derive(name, i, shift, engine="vector"):
+            col = column(name, i)
+            ratio = ratios[:, shift - 1, col:col + 1]
+            if engine == "vector":
+                nc.vector.tensor_scalar(term[name, i, shift][:, PAD:PAD + S], term[name, i, 0][:], ratio, None, ALU.mult)
+            else:
+                nc.gpsimd.tensor_scalar(term[name, i, shift][:, PAD:PAD + S], term[name, i, 0][:], ratio, 0.0, ALU.mult, ALU.add)
+
+        def direct_term(name, i, shift, engine="scalar", over=None):
+            if shift == 0:
+                term[name, i, 0] = place([P, S], F32, ROW, f"term_{name}{i}_0", over)
+                target = term[name, i, 0][:]
+            else:
+                target = term[name, i, shift][:, PAD:PAD + S]
+            if engine == "vector":
+                nc.vector.tensor_scalar(target, scores[name, i][:], tap(name, i, shift), None, ALU.mult)
+            else:
+                nc.scalar.activation(out=target, in_=scores[name, i][:], func=ACT.Copy, scale=tap(name, i, shift))
+
+        def sum_term(name, i, shift):
+            first = i not in summed
+            if first:
+                summed[i] = psum.tile([P, TILES, P], F32, name=f"summed{i}", tag=f"scores_h{i}")
+                terms_left[i] = 2 * TAPS
+            terms_left[i] = terms_left[i] - 1
+            at = PAD - shift if shift else 0
+            for b in range(TILES):
+                nc.tensor.matmul(
+                    summed[i][:, b, :],
+                    lhsT=term[name, i, shift][:, at + b * P:at + (b + 1) * P],
+                    rhs=identity[:],
+                    is_transpose=True,
+                    start=(first and b == 0),
+                    stop=(terms_left[i] == 0 and b == TILES - 1),
+                )
+
+        def turn_back(i, engine="scalar", over=None):
+            turned_sum = place([P, TILES, P], F32, ROW, f"turned_sum{i}", over)
+            if engine == "vector":
+                nc.vector.tensor_copy(out=turned_sum[:], in_=summed[i][:])
+            else:
+                nc.scalar.copy(out=turned_sum[:], in_=summed[i][:])
+            acc[i] = psum.tile([P, S], F32, name=f"sum{i}", tag=f"scores_g{i}")
+            for b in range(TILES):
+                nc.tensor.transpose(acc[i][:, b * P:(b + 1) * P], turned_sum[:, b, :], identity[:])
+
         def row_max(i, over=None):
             neg_max[i] = place([P, 1], F32, 64, f"neg_max{i}", over)
             nc.vector.tensor_reduce(out=neg_max[i][:], in_=acc[i][:], axis=AXIS.X, op=ALU.max, negate=True)
 
-        def round_scores(i):
-            rounded[i] = place([P, S], BF16, ROW, f"rounded{i}")
+        def round_scores(i, over=None):
+            rounded[i] = place([P, S], BF16, ROW, f"rounded{i}", over)
             nc.scalar.copy(out=rounded[i][:], in_=acc[i][:])
 
         def row_max_rounded(i, over=None):
@@ -252,10 +335,12 @@ def tile_picked_ymta_two_p_kernel(tc, x_words, x_scales, hT, gT, ka, kb, offs, o
         load_queries("h", 2, 2, 1)
         load_queries("g", 2, 2, 0)
         load_queries("g", 2, 2, 1)
+        clear_pads(1)
         turn_taps("scores_g3")
         gather_words(0)
         gather_scales()
         gather_words(1)
+        tap_ratios(("word_table1", 0))
         cast("h", 0, 1, 0, "vector")
         cast("h", 1, 1, 0, "scalar")
         cast("h", 2, 2, 0, "scalar")
@@ -267,51 +352,55 @@ def tile_picked_ymta_two_p_kernel(tc, x_words, x_scales, hT, gT, ka, kb, offs, o
         cast("h", 1, 1, 1, "scalar")
         quantize("h", 0, 1, 1)
         multiply("h", 0, 1)
+        cast_shared("g", 0, 0)
         quantize("h", 2, 2, 0)
         quantize("h", 1, 1, 1)
         multiply("h", 1, 1)
         multiply("h", 2, 0)
         multiply("h", 3, 0)
-        cast("g", 0, 2, 0, "scalar")
-        first_tap(0, "vector")
-        first_tap(1, "scalar", ("raw_g0_0", 0))
-        cast("g", 0, 1, 1, "scalar")
-        cast("g", 1, 1, 1, "scalar")
-        cast("h", 2, 2, 1, "scalar")
-        cast("g", 2, 2, 0, "scalar")
-        add_tap("h", 0, 1)
         quantize("g", 0, 2, 0)
         multiply("g", 0, 0)
         multiply("g", 1, 0)
-        add_tap("h", 0, 2)
-        quantize("g", 0, 1, 1)
+        first_tap(0, "scalar", ("raw_g0_0", 0))
+        cast("g", 0, 2, 1, "scalar")
+        cast("h", 2, 2, 1, "scalar")
+        add_tap("h", 0, 1)
+        quantize("g", 0, 2, 1)
         multiply("g", 0, 1)
-        add_tap("h", 1, 1)
-        quantize("g", 1, 1, 1)
         multiply("g", 1, 1)
-        add_tap("h", 1, 2)
+        base_term("h", 1, "scalar", ("raw_g0_1", 0))
+        add_tap("h", 0, 2)
         quantize("h", 2, 2, 1)
         multiply("h", 2, 1)
         multiply("h", 3, 1)
-        first_tap(2, "scalar")
+        base_term("g", 1)
+        cast("g", 2, 2, 0, "vector")
         cast("g", 2, 2, 1, "scalar")
-        first_tap(3, "scalar")
         add_tap("g", 0, 1)
-        add_tap("g", 1, 1)
-        add_tap("g", 0, 2)
         quantize("g", 2, 2, 0)
         multiply("g", 2, 0)
         multiply("g", 3, 0)
-        add_tap("g", 1, 2)
-        add_tap("h", 2, 1)
+        derive("h", 1, 1)
+        derive("h", 1, 2)
+        derive("g", 1, 1)
+        derive("g", 1, 2)
+        add_tap("g", 0, 2)
         quantize("g", 2, 2, 1)
         multiply("g", 2, 1)
         multiply("g", 3, 1)
+        first_tap(2, "scalar", ("raw_g2_1", 0))
+        first_tap(3, "scalar", ("raw_g2_1", 2048))
+        sum_term("h", 1, 0)
+        sum_term("g", 1, 0)
+        sum_term("h", 1, 1)
+        sum_term("h", 1, 2)
+        sum_term("g", 1, 1)
+        sum_term("g", 1, 2)
         side_tap("g", 0, 0, ("grouped_g2_1", 0))
+        turn_back(1)
         side_tap("g", 2, 0)
-        side_tap("g", 1, 0)
         add_side("g", 0, 0)
-        add_side("g", 1, 0)
+        add_tap("h", 2, 1)
         add_tap("h", 3, 1)
         add_tap("h", 2, 2)
         add_tap("h", 3, 2)
@@ -320,18 +409,17 @@ def tile_picked_ymta_two_p_kernel(tc, x_words, x_scales, hT, gT, ka, kb, offs, o
         add_tap("g", 2, 2)
         add_side("g", 2, 0)
         add_tap("g", 3, 1)
-        round_scores(0)
+        row_max(1)
+        exponentiate(1)
+        add_tap("g", 3, 2)
+        round_scores(0, ("turned_sum1", 0))
         row_max_rounded(0)
         exponentiate(0)
-        add_tap("g", 3, 2)
-        round_scores(1)
-        row_max_rounded(1)
-        exponentiate(1)
         row_max(3)
         exponentiate(3)
         row_max(2)
         exponentiate(2)
-        normalise(0, "gpsimd", ("side_g2_0", 0))
-        normalise(1, "vector")
+        normalise(1, "gpsimd", ("side_g2_0", 0))
+        normalise(0, "vector")
         normalise(3, "vector")
         normalise(2, "vector")

@@ -215,6 +215,10 @@ def tile_picked_ymta_two_p_kernel(tc, x_words, x_scales, hT, gT, ka, kb, offs, o
                     term[name, i, shift] = place([P, PAD + S], F32, ROW + 64, f"term_{name}{i}_{shift}")
                     nc.gpsimd.memset(term[name, i, shift][:, 0:PAD], 0.0)
 
+        def pad_term(name, i, shift, over=None):
+            term[name, i, shift] = place([P, PAD + S], F32, ROW + 64, f"term_{name}{i}_{shift}", over)
+            nc.gpsimd.memset(term[name, i, shift][:, 0:PAD], 0.0)
+
         def base_term(name, i, engine="scalar", over=None):
             term[name, i, 0] = place([P, S], F32, ROW, f"term_{name}{i}_0", over)
             col = column(name, i)
@@ -242,11 +246,11 @@ def tile_picked_ymta_two_p_kernel(tc, x_words, x_scales, hT, gT, ka, kb, offs, o
             else:
                 nc.scalar.activation(out=target, in_=scores[name, i][:], func=ACT.Copy, scale=tap(name, i, shift))
 
-        def sum_term(name, i, shift):
+        def sum_term(name, i, shift, bank=None, count=2 * TAPS):
             first = i not in summed
             if first:
-                summed[i] = psum.tile([P, TILES, P], F32, name=f"summed{i}", tag=f"scores_h{i}")
-                terms_left[i] = 2 * TAPS
+                summed[i] = psum.tile([P, TILES, P], F32, name=f"summed{i}", tag=bank or f"scores_h{i}")
+                terms_left[i] = count
             terms_left[i] = terms_left[i] - 1
             at = PAD - shift if shift else 0
             for b in range(TILES):
@@ -269,6 +273,10 @@ def tile_picked_ymta_two_p_kernel(tc, x_words, x_scales, hT, gT, ka, kb, offs, o
             for b in range(TILES):
                 nc.tensor.transpose(acc[i][:, b * P:(b + 1) * P], turned_sum[:, b, :], identity[:])
 
+        def join_sides(name, i, shift, other):
+            joined = side[name, i, shift]
+            nc.gpsimd.tensor_tensor(out=joined[:], in0=joined[:], in1=side[name, i, other][:], op=ALU.add)
+
         def row_max(i, over=None):
             neg_max[i] = place([P, 1], F32, 64, f"neg_max{i}", over)
             nc.vector.tensor_reduce(out=neg_max[i][:], in_=acc[i][:], axis=AXIS.X, op=ALU.max, negate=True)
@@ -282,9 +290,9 @@ def tile_picked_ymta_two_p_kernel(tc, x_words, x_scales, hT, gT, ka, kb, offs, o
             neg_max[i] = keep.tile([P, 1], F32, name=f"neg_max{i}")
             nc.vector.tensor_scalar(flipped[:], rounded[i][:], -1.0, None, ALU.mult, ALU.min, accum_out=neg_max[i][:])
 
-        def exponentiate(i):
+        def exponentiate(i, over=None):
             expd[i] = keep.tile([P, S], F32, name=f"expd{i}")
-            total[i] = keep.tile([P, 1], F32, name=f"total{i}")
+            total[i] = place([P, 1], F32, 64, f"total{i}", over)
             nc.scalar.activation(out=expd[i][:], in_=acc[i][:], func=ACT.Exp, bias=neg_max[i][:], accum_out=total[i][:])
 
         def invert(i, engine, over=None):
@@ -335,7 +343,9 @@ def tile_picked_ymta_two_p_kernel(tc, x_words, x_scales, hT, gT, ka, kb, offs, o
         load_queries("h", 2, 2, 1)
         load_queries("g", 2, 2, 0)
         load_queries("g", 2, 2, 1)
-        clear_pads(1)
+        clear_pads(0)
+        clear_side("g", 1, 2)
+        reserve("spare", ROW)
         turn_taps("scores_g3")
         gather_words(0)
         gather_scales()
@@ -353,73 +363,74 @@ def tile_picked_ymta_two_p_kernel(tc, x_words, x_scales, hT, gT, ka, kb, offs, o
         quantize("h", 0, 1, 1)
         multiply("h", 0, 1)
         cast_shared("g", 0, 0)
-        quantize("h", 2, 2, 0)
         quantize("h", 1, 1, 1)
         multiply("h", 1, 1)
-        multiply("h", 2, 0)
-        multiply("h", 3, 0)
+        quantize("h", 2, 2, 0)
+        base_term("h", 0, "scalar", ("raw_g0_0", 0))
         quantize("g", 0, 2, 0)
+        first_tap(1, "vector", ("raw_g0_0", 2048))
         multiply("g", 0, 0)
         multiply("g", 1, 0)
-        first_tap(0, "scalar", ("raw_g0_0", 0))
+        multiply("h", 2, 0)
+        multiply("h", 3, 0)
         cast("g", 0, 2, 1, "scalar")
         cast("h", 2, 2, 1, "scalar")
-        add_tap("h", 0, 1)
+        derive("h", 0, 1, "gpsimd")
+        derive("h", 0, 2, "gpsimd")
+        add_tap("h", 1, 1)
         quantize("g", 0, 2, 1)
         multiply("g", 0, 1)
         multiply("g", 1, 1)
-        base_term("h", 1, "scalar", ("raw_g0_1", 0))
-        add_tap("h", 0, 2)
+        sum_term("h", 0, 0)
+        sum_term("h", 0, 1)
+        sum_term("h", 0, 2)
+        add_tap("h", 1, 2)
         quantize("h", 2, 2, 1)
         multiply("h", 2, 1)
         multiply("h", 3, 1)
-        base_term("g", 1)
+        base_term("g", 0, "scalar", ("raw_h2_1", 0))
         cast("g", 2, 2, 0, "vector")
         cast("g", 2, 2, 1, "scalar")
-        add_tap("g", 0, 1)
         quantize("g", 2, 2, 0)
         multiply("g", 2, 0)
         multiply("g", 3, 0)
-        derive("h", 1, 1)
-        derive("h", 1, 2)
-        derive("g", 1, 1)
-        derive("g", 1, 2)
-        add_tap("g", 0, 2)
+        derive("g", 0, 1)
+        derive("g", 0, 2)
+        sum_term("g", 0, 0)
+        sum_term("g", 0, 1)
+        sum_term("g", 0, 2)
         quantize("g", 2, 2, 1)
         multiply("g", 2, 1)
         multiply("g", 3, 1)
+        add_tap("g", 1, 1)
         first_tap(2, "scalar", ("raw_g2_1", 0))
         first_tap(3, "scalar", ("raw_g2_1", 2048))
-        sum_term("h", 1, 0)
-        sum_term("g", 1, 0)
-        sum_term("h", 1, 1)
-        sum_term("h", 1, 2)
-        sum_term("g", 1, 1)
-        sum_term("g", 1, 2)
-        side_tap("g", 0, 0, ("grouped_g2_1", 0))
-        turn_back(1)
+        side_tap("g", 1, 0, ("grouped_g2_1", 0))
         side_tap("g", 2, 0)
-        add_side("g", 0, 0)
+        side_tap("g", 1, 2)
+        turn_back(0)
+        add_side("g", 1, 0)
+        add_side("g", 1, 2)
         add_tap("h", 2, 1)
         add_tap("h", 3, 1)
         add_tap("h", 2, 2)
         add_tap("h", 3, 2)
         add_tap("g", 2, 1)
-        add_tap("g", 3, 0)
+        add_tap("g", 3, 0, ("spare", 0))
         add_tap("g", 2, 2)
         add_side("g", 2, 0)
         add_tap("g", 3, 1)
-        row_max(1)
-        exponentiate(1)
-        add_tap("g", 3, 2)
-        round_scores(0, ("turned_sum1", 0))
-        row_max_rounded(0)
+        row_max(0, ("acc3", 0))
         exponentiate(0)
+        add_tap("g", 3, 2)
+        round_scores(1, ("turned_sum0", 0))
+        row_max_rounded(1)
+        exponentiate(1)
         row_max(3)
         exponentiate(3)
         row_max(2)
         exponentiate(2)
-        normalise(1, "gpsimd", ("side_g2_0", 0))
-        normalise(0, "vector")
+        normalise(0, "gpsimd", ("side_g2_0", 0))
+        normalise(1, "vector")
         normalise(3, "vector")
         normalise(2, "vector")

@@ -346,6 +346,7 @@ def tile_picked_ymta_two_p_kernel(tc, x_words, x_scales, hT, gT, ka, kb, offs, o
         clear_pads(0)
         clear_side("g", 1, 2)
         reserve("spare", ROW)
+        reserve("lastcodes", ROW)
         turn_taps("scores_g3")
         gather_words(0)
         gather_scales()
@@ -390,7 +391,7 @@ def tile_picked_ymta_two_p_kernel(tc, x_words, x_scales, hT, gT, ka, kb, offs, o
         multiply("h", 3, 1)
         base_term("g", 0, "scalar", ("raw_h2_1", 0))
         cast("g", 2, 2, 0, "vector")
-        cast("g", 2, 2, 1, "scalar")
+        cast_shared("g", 2, 1)
         quantize("g", 2, 2, 0)
         multiply("g", 2, 0)
         multiply("g", 3, 0)
@@ -399,7 +400,7 @@ def tile_picked_ymta_two_p_kernel(tc, x_words, x_scales, hT, gT, ka, kb, offs, o
         sum_term("g", 0, 0)
         sum_term("g", 0, 1)
         sum_term("g", 0, 2)
-        quantize("g", 2, 2, 1)
+        quantize("g", 2, 2, 1, ("lastcodes", 0))
         multiply("g", 2, 1)
         multiply("g", 3, 1)
         add_tap("g", 1, 1)
@@ -408,7 +409,7 @@ def tile_picked_ymta_two_p_kernel(tc, x_words, x_scales, hT, gT, ka, kb, offs, o
         side_tap("g", 1, 0, ("grouped_g2_1", 0))
         side_tap("g", 2, 0)
         side_tap("g", 1, 2)
-        turn_back(0)
+        turn_back(0, "scalar", ("lastcodes", 0))
         add_side("g", 1, 0)
         add_side("g", 1, 2)
         add_tap("h", 2, 1)

@@ -118,8 +118,8 @@ def tile_picked_ymta_two_p_kernel(tc, x_words, x_scales, hT, gT, ka, kb, offs, o
                 nc.scalar.copy(out=dst, in_=src)
             grouped[name, first, o] = tile
 
-        def cast_shared(name, first, o):
-            tile = place([P, 2 * P, PACK], BF16, ROW, f"grouped_{name}{first}_{o}")
+        def cast_shared(name, first, o, over=None):
+            tile = place([P, 2 * P, PACK], BF16, ROW, f"grouped_{name}{first}_{o}", over)
             loaded, at = raw[name, first, o]
             for m, copy in enumerate((nc.vector.tensor_copy, nc.scalar.copy)):
                 dst = tile[:, m * P:(m + 1) * P, :].rearrange("p (c i) t -> p c t i", i=RUN)
@@ -281,6 +281,11 @@ def tile_picked_ymta_two_p_kernel(tc, x_words, x_scales, hT, gT, ka, kb, offs, o
             neg_max[i] = place([P, 1], F32, 64, f"neg_max{i}", over)
             nc.vector.tensor_reduce(out=neg_max[i][:], in_=acc[i][:], axis=AXIS.X, op=ALU.max, negate=True)
 
+        def row_max_streamed(i):
+            flipped = place([P, S], BF16, ROW // 2, f"flipped{i}")
+            neg_max[i] = keep.tile([P, 1], F32, name=f"neg_max{i}")
+            nc.vector.tensor_scalar(flipped[:], acc[i][:], -1.0, None, ALU.mult, ALU.min, accum_out=neg_max[i][:])
+
         def round_scores(i, over=None):
             rounded[i] = place([P, S], BF16, ROW, f"rounded{i}", over)
             nc.scalar.copy(out=rounded[i][:], in_=acc[i][:])
@@ -354,7 +359,7 @@ def tile_picked_ymta_two_p_kernel(tc, x_words, x_scales, hT, gT, ka, kb, offs, o
         tap_ratios(("word_table1", 0))
         cast("h", 0, 1, 0, "vector")
         cast("h", 1, 1, 0, "scalar")
-        cast("h", 2, 2, 0, "scalar")
+        cast_shared("h", 2, 0)
         quantize("h", 0, 1, 0)
         multiply("h", 0, 0)
         quantize("h", 1, 1, 0)
@@ -366,7 +371,7 @@ def tile_picked_ymta_two_p_kernel(tc, x_words, x_scales, hT, gT, ka, kb, offs, o
         cast_shared("g", 0, 0)
         quantize("h", 1, 1, 1)
         multiply("h", 1, 1)
-        quantize("h", 2, 2, 0)
+        quantize("h", 2, 2, 0, ("grouped_h1_1", 0))
         base_term("h", 0, "scalar", ("raw_g0_0", 0))
         quantize("g", 0, 2, 0)
         first_tap(1, "vector", ("raw_g0_0", 2048))

@@ -348,9 +348,12 @@ def tile_picked_ymta_two_p_kernel(tc, x_words, x_scales, hT, gT, ka, kb, offs, o
         load_queries("h", 2, 2, 1)
         load_queries("g", 2, 2, 0)
         load_queries("g", 2, 2, 1)
-        clear_pads(0)
+        pad_term("h", 0, 1)
+        pad_term("g", 0, 1)
+        reserve("last", 3 * ROW + 64)
         clear_side("g", 1, 2)
         reserve("spare", ROW)
+        reserve("wide", ROW + 64)
         reserve("lastcodes", ROW)
         turn_taps("scores_g3")
         gather_words(0)
@@ -379,39 +382,41 @@ def tile_picked_ymta_two_p_kernel(tc, x_words, x_scales, hT, gT, ka, kb, offs, o
         multiply("g", 1, 0)
         multiply("h", 2, 0)
         multiply("h", 3, 0)
-        cast("g", 0, 2, 1, "scalar")
+        cast("g", 0, 2, 1, "scalar", ("wide", 0))
         cast("h", 2, 2, 1, "scalar")
         derive("h", 0, 1, "gpsimd")
-        derive("h", 0, 2, "gpsimd")
         add_tap("h", 1, 1)
         quantize("g", 0, 2, 1)
         multiply("g", 0, 1)
         multiply("g", 1, 1)
-        sum_term("h", 0, 0)
-        sum_term("h", 0, 1)
-        sum_term("h", 0, 2)
         add_tap("h", 1, 2)
         quantize("h", 2, 2, 1)
         multiply("h", 2, 1)
         multiply("h", 3, 1)
+        sum_term("h", 0, 0)
+        sum_term("h", 0, 1)
+        pad_term("h", 0, 2, ("wide", 0))
+        derive("h", 0, 2, "gpsimd")
+        sum_term("h", 0, 2)
         base_term("g", 0, "scalar", ("raw_h2_1", 0))
         cast("g", 2, 2, 0, "vector")
-        cast_shared("g", 2, 1)
+        cast_shared("g", 2, 1, ("last", ROW))
         quantize("g", 2, 2, 0)
         multiply("g", 2, 0)
         multiply("g", 3, 0)
         derive("g", 0, 1)
-        derive("g", 0, 2)
-        sum_term("g", 0, 0)
-        sum_term("g", 0, 1)
-        sum_term("g", 0, 2)
         quantize("g", 2, 2, 1, ("lastcodes", 0))
         multiply("g", 2, 1)
         multiply("g", 3, 1)
         add_tap("g", 1, 1)
         first_tap(2, "scalar", ("raw_g2_1", 0))
         first_tap(3, "scalar", ("raw_g2_1", 2048))
-        side_tap("g", 1, 0, ("grouped_g2_1", 0))
+        pad_term("g", 0, 2, ("last", 2 * ROW - 64))
+        derive("g", 0, 2, "gpsimd")
+        sum_term("g", 0, 0)
+        sum_term("g", 0, 1)
+        sum_term("g", 0, 2)
+        side_tap("g", 1, 0, ("last", 64))
         side_tap("g", 2, 0)
         side_tap("g", 1, 2)
         turn_back(0, "scalar", ("lastcodes", 0))

@@ -400,16 +400,17 @@ def tile_picked_ymta_two_p_kernel(tc, x_words, x_scales, hT, gT, ka, kb, offs, o
         sum_term("h", 0, 2)
         base_term("g", 0, "scalar", ("raw_h2_1", 0))
         cast("g", 2, 2, 0, "vector")
+        first_tap(2, "scalar", ("raw_h2_1", 2048))
         cast_shared("g", 2, 1, ("last", ROW))
         quantize("g", 2, 2, 0)
         multiply("g", 2, 0)
         multiply("g", 3, 0)
         derive("g", 0, 1)
+        add_tap("g", 1, 1)
+        add_tap("h", 2, 1)
         quantize("g", 2, 2, 1, ("lastcodes", 0))
         multiply("g", 2, 1)
         multiply("g", 3, 1)
-        add_tap("g", 1, 1)
-        first_tap(2, "scalar", ("raw_g2_1", 0))
         first_tap(3, "scalar", ("raw_g2_1", 2048))
         pad_term("g", 0, 2, ("last", 2 * ROW - 64))
         derive("g", 0, 2, "gpsimd")
@@ -422,9 +423,8 @@ def tile_picked_ymta_two_p_kernel(tc, x_words, x_scales, hT, gT, ka, kb, offs, o
         turn_back(0, "scalar", ("lastcodes", 0))
         add_side("g", 1, 0)
         add_side("g", 1, 2)
-        add_tap("h", 2, 1)
-        add_tap("h", 3, 1)
         add_tap("h", 2, 2)
+        add_tap("h", 3, 1)
         add_tap("h", 3, 2)
         add_tap("g", 2, 1)
         add_tap("g", 3, 0, ("spare", 0))

from contextlib import ExitStack

import concourse.mybir as mybir
from concourse.masks import make_identity

F32 = mybir.dt.float32
BF16 = mybir.dt.bfloat16
I32 = mybir.dt.int32
U32 = mybir.dt.uint32
U16 = mybir.dt.uint16
U8 = mybir.dt.uint8
FP8X4 = mybir.dt.float8_e4m3fn_x4
ALU = mybir.AluOpType
ACT = mybir.ActivationFunctionType
AXIS = mybir.AxisListType

K, T, S, V = 1024, 2048, 512, 512
P = 128
PACK = 4
K_PASS = P * PACK
PASSES = K // K_PASS
TILES = V // P
TAPS = 3
RUN = 2
ROW = 4 * S
PAD = 8
NUDGE = 2.0 ** -64
FLOPS = 2 * 2 * K * S * V


def tile_picked_ymta_two_p_kernel(tc, x_words, x_scales, hT, gT, ka, kb, offs, out):
    nc = tc.nc
    with ExitStack() as ctx:
        keep = ctx.enter_context(tc.tile_pool(name="keep", bufs=1))
        psum = ctx.enter_context(tc.psum_pool(name="psum", bufs=1))

        work = ctx.enter_context(tc.tile_pool(name="work", bufs=1))
        start_of = {}
        free_from = [0]

        def place(shape, dtype, width, name, over=None):
            if over is None:
                start_of[name] = free_from[0]
                free_from[0] = free_from[0] + width
            else:
                start_of[name] = start_of[over[0]] + over[1]
            return work.tile(shape, dtype, name=name, offset=start_of[name], align_bytes=64)

        def reserve(name, width):
            start_of[name] = free_from[0]
            free_from[0] = free_from[0] + width

        offsets = keep.tile([P, S // 16], U16, name="offsets")
        word_table = [place([P, T], I32, 4 * T, f"word_table{o}") for o in range(PASSES)]
        scale_table = place([P, T], U8, T, "scale_table")
        key_words = [keep.tile([P, S], U32, name=f"key_words{o}", align_bytes=64) for o in range(PASSES)]
        key_scales = keep.tile([P, S], U8, name="key_scales", align_bytes=64)
        tap_rows = keep.tile([P, P * TAPS], F32, name="tap_rows")
        taps = keep.tile([P, TAPS, 2 * TILES], F32, name="taps")
        identity = keep.tile([P, P], F32, name="identity")
        warm = keep.tile([P, 8], F32, name="warm")
        warm_out = keep.tile([P, 8], F32, name="warm_out")

        raw, grouped, codes, scales, scores, acc, side = {}, {}, {}, {}, {}, {}, {}
        term, summed, terms_left = {}, {}, {}
        nudge = keep.tile([P, 2 * TILES], F32, name="nudge")
        pivot = keep.tile([P, 2 * TILES], F32, name="pivot")
        raised = keep.tile([P, 2 * TILES], F32, name="raised")
        ratios = keep.tile([P, TAPS - 1, 2 * TILES], F32, name="ratios")
        rounded, neg_max, expd, total, inv = {}, {}, {}, {}, {}

        def load_list():
            nc.sync.dma_start(offsets[:], offs)

        def load_queries(name, first, count, o):
            src = hT if name == "h" else gT
            tile = place([P, PACK, count * P], F32, 4 * PACK * count * P, f"raw_{name}{first}_{o}")
            rows = src[o * K_PASS:(o + 1) * K_PASS, first * P:(first + count) * P]
            nc.sync.dma_start(out=tile[:], in_=rows.rearrange("(p j) w -> p j w", j=PACK))
            for m in range(count):
                raw[name, first + m, o] = (tile, m * P)

        def load_words(o):
            nc.sync.dma_start(out=word_table[o][:], in_=x_words[o].rearrange("p n t -> p (n t)").bitcast(I32))

        def load_scales(queue):
            for q in range(4):
                queue.dma_start(
                    out=scale_table[32 * q:32 * q + 4 * PASSES, :].bitcast(I32),
                    in_=x_scales[:, 4 * q:4 * q + 4, :].bitcast(I32),
                )

        def load_taps():
            nc.sync.dma_start(out=tap_rows[0:4 * TILES:4, :], in_=ka.rearrange("(i p) c -> i (p c)", p=P))
            nc.sync.dma_start(out=tap_rows[4 * TILES:8 * TILES:4, :], in_=kb.rearrange("(i p) c -> i (p c)", p=P))

        def turn_taps(bank):
            turned = psum.tile([P, TAPS, P], F32, name="turned", tag=bank)
            for c in range(TAPS):
                nc.tensor.transpose(turned[:, c, :], tap_rows[:, c::TAPS], identity[:])
            nc.scalar.copy(out=taps[:], in_=turned[:, :, 0:8 * TILES:4])

        def tap(name, i, shift):
            col = i if name == "h" else TILES + i
            return taps[:, shift, col:col + 1]

        def cast(name, first, count, o, engine, over=None):
            tile = place([P, count * P, PACK], BF16, ROW, f"grouped_{name}{first}_{o}", over)
            loaded, at = raw[name, first, o]
            rows = loaded[:, :, at:at + count * P]
            dst = tile[:].rearrange("p (c i) t -> p c t i", i=RUN)
            src = rows.rearrange("p t (c i) -> p c t i", i=RUN)
            if engine == "vector":
                nc.vector.tensor_copy(out=dst, in_=src)
            elif engine == "gpsimd":
                nc.gpsimd.tensor_scalar(tile[:], rows.rearrange("p t w -> p w t"), 1.0, 0.0, ALU.mult, ALU.add)
            else:
                nc.scalar.copy(out=dst, in_=src)
            grouped[name, first, o] = tile

        def cast_shared(name, first, o, over=None):
            tile = place([P, 2 * P, PACK], BF16, ROW, f"grouped_{name}{first}_{o}", over)
            loaded, at = raw[name, first, o]
            for m, copy in enumerate((nc.vector.tensor_copy, nc.scalar.copy)):
                dst = tile[:, m * P:(m + 1) * P, :].rearrange("p (c i) t -> p c t i", i=RUN)
                src = loaded[:, :, at + m * P:at + (m + 1) * P].rearrange("p t (c i) -> p c t i", i=RUN)
                copy(out=dst, in_=src)
            grouped[name, first, o] = tile

        def quantize(name, first, count, o, over=None):
            words = place([P, count * P], U32, 4 * count * P, f"codes_{name}{first}_{o}", over)
            plane = keep.tile([P, count * P], U8, name=f"scales_{name}{first}_{o}", align_bytes=64)
            nc.vector.quantize_mx(
                out=words[:].bitcast(FP8X4),
                scales=plane[:],
                in_=grouped[name, first, o][:].rearrange("p w t -> p (w t)"),
            )
            for i in range(first, first + count):
                cols = slice((i - first) * P, (i - first + 1) * P)
                codes[name, i, o] = words[:, cols]
                scales[name, i, o] = plane[:, cols]

        def multiply(name, i, o):
            if o == 0:
                scores[name, i] = psum.tile([P, S], F32, name=f"scores_{name}{i}", tag=f"scores_{name}{i}")
            nc.tensor.matmul_mx(
                out=scores[name, i][:],
                lhsT=codes[name, i, o].bitcast(FP8X4),
                lhsT_scale=scales[name, i, o],
                rhs=key_words[o][:].bitcast(FP8X4),
                rhs_scale=key_scales[4 * o:P, :],
                start=(o == 0),
                stop=(o == PASSES - 1),
            )

        def first_tap(i, engine, over=None):
            acc[i] = place([P, S], F32, ROW, f"acc{i}", over)
            if engine == "vector":
                nc.vector.tensor_scalar(acc[i][:], scores["h", i][:], tap("h", i, 0), None, ALU.mult)
            else:
                nc.scalar.activation(out=acc[i][:], in_=scores["h", i][:], func=ACT.Copy, scale=tap("h", i, 0))

        def add_tap(name, i, shift, over=None):
            before = acc[i]
            if over is not None:
                acc[i] = place([P, S], F32, ROW, f"moved_{name}{i}", over)
            nc.vector.scalar_tensor_tensor(
                out=acc[i][:, shift:S],
                in0=scores[name, i][:, 0:S - shift],
                scalar=tap(name, i, shift),
                in1=before[:, shift:S],
                op0=ALU.mult,
                op1=ALU.add,
            )

        def clear_side(name, i, shift):
            side[name, i, shift] = place([P, S], F32, ROW, f"side_{name}{i}_{shift}")
            nc.gpsimd.memset(side[name, i, shift][:, 0:shift], 0.0)

        def side_tap(name, i, shift, over=None):
            if shift == 0:
                side[name, i, shift] = place([P, S], F32, ROW, f"side_{name}{i}_{shift}", over)
            nc.scalar.activation(
                out=side[name, i, shift][:, shift:S],
                in_=scores[name, i][:, 0:S - shift],
                func=ACT.Copy,
                scale=tap(name, i, shift),
            )

        def add_side(name, i, shift, over=None):
            before = acc[i]
            if over is not None:
                acc[i] = place([P, S], F32, ROW, f"joined_{name}{i}_{shift}", over)
            nc.gpsimd.tensor_tensor(out=acc[i][:], in0=before[:], in1=side[name, i, shift][:], op=ALU.add)

        def tap_ratios(over=None):
            nc.gpsimd.tensor_scalar(nudge[:], taps[:, 0, :], 0.0, 2.0 * NUDGE, ALU.is_ge, ALU.mult)
            nc.gpsimd.tensor_tensor(out=raised[:], in0=nudge[:], in1=taps[:, 0, :], op=ALU.add)
            nc.gpsimd.tensor_scalar(pivot[:], raised[:], 1.0, -NUDGE, ALU.mult, ALU.add)
            inv_pivot = place([P, 2 * TILES], F32, 64, "inv_pivot", over)
            nc.vector.reciprocal(out=inv_pivot[:], in_=pivot[:])
            nc.gpsimd.tensor_tensor(
                out=ratios[:],
                in0=taps[:, 1:TAPS, :],
                in1=inv_pivot[:].unsqueeze(1).to_broadcast([P, TAPS - 1, 2 * TILES]),
                op=ALU.mult,
            )

        def column(name, i):
            return i if name == "h" else TILES + i

        def clear_pads(i):
            for name in ("h", "g"):
                for shift in range(1, TAPS):
                    term[name, i, shift] = place([P, PAD + S], F32, ROW + 64, f"term_{name}{i}_{shift}")
                    nc.gpsimd.memset(term[name, i, shift][:, 0:PAD], 0.0)

        def pad_term(name, i, shift, over=None):
            term[name, i, shift] = place([P, PAD + S], F32, ROW + 64, f"term_{name}{i}_{shift}", over)
            nc.gpsimd.memset(term[name, i, shift][:, 0:PAD], 0.0)

        def base_term(name, i, engine="scalar", over=None):
            term[name, i, 0] = place([P, S], F32, ROW, f"term_{name}{i}_0", over)
            col = column(name, i)
            if engine == "vector":
                nc.vector.tensor_scalar(term[name, i, 0][:], scores[name, i][:], pivot[:, col:col + 1], None, ALU.mult)
            else:
                nc.scalar.activation(out=term[name, i, 0][:], in_=scores[name, i][:], func=ACT.Copy, scale=pivot[:, col:col + 1])

        def derive(name, i, shift, engine="vector"):
            col = column(name, i)
            ratio = ratios[:, shift - 1, col:col + 1]
            if engine == "vector":
                nc.vector.tensor_scalar(term[name, i, shift][:, PAD:PAD + S], term[name, i, 0][:], ratio, None, ALU.mult)
            else:
                nc.gpsimd.tensor_scalar(term[name, i, shift][:, PAD:PAD + S], term[name, i, 0][:], ratio, 0.0, ALU.mult, ALU.add)

        def direct_term(name, i, shift, engine="scalar", over=None):
            if shift == 0:
                term[name, i, 0] = place([P, S], F32, ROW, f"term_{name}{i}_0", over)
                target = term[name, i, 0][:]
            else:
                target = term[name, i, shift][:, PAD:PAD + S]
            if engine == "vector":
                nc.vector.tensor_scalar(target, scores[name, i][:], tap(name, i, shift), None, ALU.mult)
            else:
                nc.scalar.activation(out=target, in_=scores[name, i][:], func=ACT.Copy, scale=tap(name, i, shift))

        def sum_term(name, i, shift, bank=None, count=2 * TAPS):
            first = i not in summed
            if first:
                summed[i] = psum.tile([P, TILES, P], F32, name=f"summed{i}", tag=bank or f"scores_h{i}")
                terms_left[i] = count
            terms_left[i] = terms_left[i] - 1
            at = PAD - shift if shift else 0
            for b in range(TILES):
                nc.tensor.matmul(
                    summed[i][:, b, :],
                    lhsT=term[name, i, shift][:, at + b * P:at + (b + 1) * P],
                    rhs=identity[:],
                    is_transpose=True,
                    start=(first and b == 0),
                    stop=(terms_left[i] == 0 and b == TILES - 1),
                )

        def turn_back(i, engine="scalar", over=None):
            turned_sum = place([P, TILES, P], F32, ROW, f"turned_sum{i}", over)
            if engine == "vector":
                nc.vector.tensor_copy(out=turned_sum[:], in_=summed[i][:])
            else:
                nc.scalar.copy(out=turned_sum[:], in_=summed[i][:])
            acc[i] = psum.tile([P, S], F32, name=f"sum{i}", tag=f"scores_g{i}")
            for b in range(TILES):
                nc.tensor.transpose(acc[i][:, b * P:(b + 1) * P], turned_sum[:, b, :], identity[:])

        def join_sides(name, i, shift, other):
            joined = side[name, i, shift]
            nc.gpsimd.tensor_tensor(out=joined[:], in0=joined[:], in1=side[name, i, other][:], op=ALU.add)

        def row_max(i, over=None):
            neg_max[i] = place([P, 1], F32, 64, f"neg_max{i}", over)
            nc.vector.tensor_reduce(out=neg_max[i][:], in_=acc[i][:], axis=AXIS.X, op=ALU.max, negate=True)

        def row_max_streamed(i):
            flipped = place([P, S], BF16, ROW // 2, f"flipped{i}")
            neg_max[i] = keep.tile([P, 1], F32, name=f"neg_max{i}")
            nc.vector.tensor_scalar(flipped[:], acc[i][:], -1.0, None, ALU.mult, ALU.min, accum_out=neg_max[i][:])

        def round_scores(i, over=None):
            rounded[i] = place([P, S], BF16, ROW, f"rounded{i}", over)
            nc.scalar.copy(out=rounded[i][:], in_=acc[i][:])

        def row_max_rounded(i, over=None):
            flipped = place([P, S], BF16, ROW // 2, f"flipped{i}", over)
            neg_max[i] = keep.tile([P, 1], F32, name=f"neg_max{i}")
            nc.vector.tensor_scalar(flipped[:], rounded[i][:], -1.0, None, ALU.mult, ALU.min, accum_out=neg_max[i][:])

        def exponentiate(i, over=None):
            expd[i] = keep.tile([P, S], F32, name=f"expd{i}")
            total[i] = place([P, 1], F32, 64, f"total{i}", over)
            nc.scalar.activation(out=expd[i][:], in_=acc[i][:], func=ACT.Exp, bias=neg_max[i][:], accum_out=total[i][:])

        def invert(i, engine, over=None):
            inv[i] = place([P, 1], F32, 64, f"inv{i}", over)
            if engine == "gpsimd":
                nc.gpsimd.tensor_tensor(out=inv[i][:], in0=total[i][:], in1=minus_one[:], op=ALU.pow)
            else:
                nc.vector.reciprocal(out=inv[i][:], in_=total[i][:])

        def scale_and_store(i, engine, over=None):
            result = place([P, S], F32, ROW, f"result{i}", over)
            if engine == "gpsimd":
                nc.gpsimd.tensor_scalar(result[:], expd[i][:], inv[i][:], 0.0, ALU.mult, ALU.add)
            elif engine == "vector":
                nc.vector.tensor_scalar(result[:], expd[i][:], inv[i][:], None, ALU.mult)
            else:
                nc.scalar.activation(out=result[:], in_=expd[i][:], func=ACT.Copy, scale=inv[i][:])
            nc.sync.dma_start(out=out[i * P:(i + 1) * P, :], in_=result[:])

        def normalise(i, engine, over=None):
            invert(i, engine, over)
            scale_and_store(i, engine)

        def gather_words(o):
            nc.vector.tensor_copy(key_words[o][:], word_table[o][:].bitcast(U32).indirect(offsets[:]))

        def gather_scales():
            nc.vector.tensor_copy(key_scales[:], scale_table[:].indirect(offsets[:]))

        minus_one = keep.tile([P, 1], F32, name="minus_one")

        nc.gpsimd.memset(tap_rows[:], 0.0)
        nc.vector.memset(scale_table[:, 0:T // 2].bitcast(I32), 0)
        nc.gpsimd.memset(scale_table[:, T // 2:T].bitcast(I32), 0)
        nc.vector.memset(warm[:], 0.0)
        nc.gpsimd.memset(minus_one[:], -1.0)
        make_identity(nc, identity[:])
        nc.scalar.activation(out=warm_out[:], in_=warm[:], func=ACT.Exp)
        load_list()
        load_words(0)
        load_taps()
        load_scales(nc.sync)
        load_words(1)
        load_queries("h", 0, 4, 0)
        load_queries("h", 0, 2, 1)
        load_queries("g", 0, 2, 0)
        load_queries("g", 0, 2, 1)
        load_queries("h", 2, 2, 1)
        load_queries("g", 2, 2, 0)
        load_queries("g", 2, 2, 1)
        pad_term("h", 0, 1)
        pad_term("g", 0, 1)
        reserve("last", 3 * ROW + 64)
        clear_side("g", 1, 2)
        reserve("spare", ROW)
        reserve("wide", ROW + 64)
        reserve("lastcodes", ROW)
        turn_taps("scores_g3")
        gather_words(0)
        gather_scales()
        gather_words(1)
        tap_ratios(("word_table1", 0))
        cast("h", 0, 1, 0, "vector")
        cast("h", 1, 1, 0, "scalar")
        cast_shared("h", 2, 0)
        quantize("h", 0, 1, 0)
        multiply("h", 0, 0)
        quantize("h", 1, 1, 0)
        multiply("h", 1, 0)
        cast("h", 0, 1, 1, "vector")
        cast("h", 1, 1, 1, "scalar")
        quantize("h", 0, 1, 1)
        multiply("h", 0, 1)
        cast_shared("g", 0, 0)
        quantize("h", 1, 1, 1)
        multiply("h", 1, 1)
        quantize("h", 2, 2, 0, ("grouped_h1_1", 0))
        base_term("h", 0, "scalar", ("raw_g0_0", 0))
        quantize("g", 0, 2, 0)
        first_tap(1, "vector", ("raw_g0_0", 2048))
        multiply("g", 0, 0)
        multiply("g", 1, 0)
        multiply("h", 2, 0)
        multiply("h", 3, 0)
        cast("g", 0, 2, 1, "scalar", ("wide", 0))
        cast("h", 2, 2, 1, "scalar")
        derive("h", 0, 1, "gpsimd")
        add_tap("h", 1, 1)
        quantize("g", 0, 2, 1)
        multiply("g", 0, 1)
        multiply("g", 1, 1)
        add_tap("h", 1, 2)
        quantize("h", 2, 2, 1)
        multiply("h", 2, 1)
        multiply("h", 3, 1)
        sum_term("h", 0, 0)
        sum_term("h", 0, 1)
        pad_term("h", 0, 2, ("wide", 0))
        derive("h", 0, 2, "gpsimd")
        sum_term("h", 0, 2)
        base_term("g", 0, "scalar", ("raw_h2_1", 0))
        cast("g", 2, 2, 0, "vector")
        first_tap(2, "scalar", ("raw_h2_1", 2048))
        cast_shared("g", 2, 1, ("last", ROW))
        quantize("g", 2, 2, 0)
        multiply("g", 2, 0)
        multiply("g", 3, 0)
        derive("g", 0, 1)
        add_tap("g", 1, 1)
        add_tap("h", 2, 1)
        quantize("g", 2, 2, 1, ("lastcodes", 0))
        multiply("g", 2, 1)
        multiply("g", 3, 1)
        first_tap(3, "scalar", ("raw_g2_1", 2048))
        pad_term("g", 0, 2, ("last", 2 * ROW - 64))
        derive("g", 0, 2, "gpsimd")
        sum_term("g", 0, 0)
        sum_term("g", 0, 1)
        sum_term("g", 0, 2)
        side_tap("g", 1, 0, ("last", 64))
        side_tap("g", 2, 0)
        side_tap("g", 1, 2)
        turn_back(0, "scalar", ("lastcodes", 0))
        add_side("g", 1, 0)
        add_side("g", 1, 2)
        add_tap("h", 2, 2)
        add_tap("h", 3, 1)
        add_tap("h", 3, 2)
        add_tap("g", 2, 1)
        add_tap("g", 3, 0, ("spare", 0))
        add_tap("g", 2, 2)
        add_side("g", 2, 0)
        add_tap("g", 3, 1)
        row_max(0, ("acc3", 0))
        exponentiate(0)
        add_tap("g", 3, 2)
        round_scores(1, ("turned_sum0", 0))
        row_max_rounded(1)
        exponentiate(1)
        row_max(3)
        exponentiate(3)
        row_max(2)
        exponentiate(2)
        normalise(0, "gpsimd", ("side_g2_0", 0))
        normalise(1, "vector")
        normalise(3, "vector")
        normalise(2, "vector")
